import numpy as np, ml_dtypes
CORES = [5,29,101,125,133,157,229,253]
N = 8
import mx_ref
BF = ml_dtypes.bfloat16
def pick(q, e):
    c = np.concatenate([q[0].reshape(128, -1, 4), np.zeros((128, 1, 4), np.uint8)], axis=1); s = np.concatenate([q[1], np.ones((16, 1), np.uint8)], axis=1)
    return (np.ascontiguousarray(c[:, e].reshape(128, -1)), np.ascontiguousarray(s[:, e]))
def join(*qs):
    return (np.concatenate([q[0] for q in qs], axis=1), np.concatenate([q[1] for q in qs], axis=1))
def put(q, e, v):
    c, s = q[0].reshape(128, -1, 4).copy(), q[1].copy(); c[:, e] = v[0].reshape(128, -1, 4); s[:, e] = v[1]
    return (c.reshape(128, -1), s)
def pk(c, s):
    return (np.ascontiguousarray(c), mx_ref.live(s))
def emit(q):
    return q[0], q[1]
def decode(q):
    o = []
    for b in range(4):
        e = np.zeros((128, 128, 4), np.float32); e[np.arange(128), np.arange(128), b] = 1
        o.append(mx_ref.matmul(mx_ref.quantize(e.reshape(128, 512).astype(BF)), q))
    return np.stack(o, axis=2).reshape(128, -1)
def cut(t, i, w=512):
    return t[:, w * i:w * i + w]
def f(rng, *shape):
    return mx_ref.flush((rng.standard_normal(shape, dtype=np.float32) * np.exp2(rng.integers(-2, 3, shape[:-1] + (1,)))).astype(BF))
def wide(rng, *shape, cols=0):
    v = rng.standard_normal(shape, dtype=np.float32) * np.exp2(rng.integers(-12, 13, shape)).astype(np.float32)
    if cols: v *= np.repeat(np.exp2(rng.integers(-cols, cols + 1, shape[:-2] + (1, shape[-1] // 4))) * (rng.random(shape[:-2] + (1, shape[-1] // 4)) > 0.0625), 4, axis=-1).astype(np.float32)
    return mx_ref.flush(v.astype(BF))
P, K, O, L = 256, 64, 1, 3
def times(t, v):
    v = t.astype(np.float32) * np.asarray(v, np.float32)
    return np.where(np.abs(v) < 2.0 ** -16, 0, v).astype(np.float32).astype(BF)
def loud(u, e):
    v = u.astype(np.float32) * np.float32(2.0 ** e)
    return np.where(np.abs(v) < 2.0 ** -30, 0, v).astype(np.float32).astype(BF)
def strong(rng, u, n):
    return np.sign(u[0, :, None, :4].astype(np.float32)) * (1 + rng.random((128, n, 4))) * 128
def near(rng, u):
    ku, v = mx_ref.quantize(np.ascontiguousarray(u[0])), np.repeat(strong(rng, u, 1), 12, axis=1).astype(np.float32)
    v[127] = 0
    z = size(ku, mx_ref.quantize(np.ascontiguousarray(v.reshape(128, -1).astype(BF))))
    v[127, 1:, 0] = np.exp2(np.floor(np.log2(z[0])) - 23 + np.arange(11))
    z = size(ku, mx_ref.quantize(np.ascontiguousarray(v.reshape(128, -1).astype(BF))))
    return v[:, [0, int(np.argmax(z > z[0]))]]
def plain(rng):
    k = np.exp2(6 * rng.random(P) - 3) * np.exp2(rng.random((N, P)) - 0.5)
    u = np.zeros((N, 128, 512), BF)
    u[:, :, :4] = f(rng, 128, 4)
    return {"gr": times(f(rng, N, 128, 4 * P), np.repeat(k, 4, axis=1)[:, None]), "u": u, "w": f(rng, N, 128, 512 * O)}
def setup_inputs(rng):
    return plain(rng)
def setup_inputs_apart(rng):
    d, h = plain(rng), K // 2
    d["u"][:, :8] = 0
    d["u"][:, 120:] = 0
    d["u"][:, 127, 0] = 1
    g = d["gr"].astype(np.float32).reshape(N, 128, P, 4) * np.float32(2.0 ** -8)
    x = rng.permutation(P)[:N // 2 * K].reshape(N // 2, 2, h)
    c = near(rng, d["u"])
    for j in range(N // 2):
        rest = rng.permutation(np.setdiff1d(np.arange(P), x[j].reshape(-1)))[:K].reshape(2, h)
        for i in range(2):
            v = c[:, (x[j, i] >= P // 2).astype(int)]
            v[:8] = (1 + rng.random((8, h, 4))) * 128 * rng.choice([-1.0, 1.0], (8, h, 4))
            g[2 * j + i][:, x[j, i]] = v * np.exp2(rng.integers(0, 3, h))[:, None]
            g[2 * j + i][:, rest[i]] = strong(rng, d["u"], h) * 2.0 ** -4
    d["gr"] = times(g.reshape(N, 128, -1), 1)
    return d
def setup_inputs_cancel(rng):
    d, m = plain(rng), K // 8
    g = d["gr"].astype(np.float32).reshape(N, 128, P, 4)
    e = rng.permutation(P)[:3 * L * m].reshape(L, 3, m)
    g[:, :, e.reshape(-1)] = 0
    for b in range(L):
        for r in range(N):
            h = (r >> b) & 1
            g[r][:, e[b, 1 + h]] = strong(rng, d["u"], m)
            if r % (1 << b) == 0:
                g[r][:, e[b, 0]] = -g[r - (1 << b)][:, e[b, 0]] if h else strong(rng, d["u"], m)
    d["gr"] = times(g.reshape(N, 128, -1), 2.0 ** -10)
    d["u"] = loud(d["u"], -26)
    return d
def setup_inputs_few(rng):
    d, m, h = plain(rng), K // 8, N // 2
    d["u"][:, :64] = 0
    g = d["gr"].astype(np.float32).reshape(N, 128, P, 4)
    g[:, 64:] = 0
    g *= (np.arange(P) % 4 != rng.integers(0, 4, (N, 1)))[:, None, :, None]
    low, e = rng.permutation(K // 4)[:m], K + rng.permutation(P - K)[:(h + 3) * m].reshape(h + 3, m)
    c = np.concatenate([low, e[0]])
    for r in range(N):
        own = e[3 + r] if r < h else e[1:3].reshape(-1)
        g[r][:, own] += strong(rng, d["u"], own.size)
        if r % 2: g[r][:, c] = -g[r - 1][:, c]
        else: g[r][:, c] += strong(rng, d["u"], c.size)
    d["gr"] = times(g.reshape(N, 128, -1), 1)
    d["u"] = loud(d["u"], 24)
    return d
def setup_inputs_spread(rng):
    d = plain(rng)
    e = rng.permutation(P)[:K]
    k = np.exp2(rng.integers(-12, -5, (N, P))) * (rng.random((N, P)) > 0.0625)
    k[:, e] = np.exp2(rng.integers(0, 7, (N, K))) * rng.choice([-1.0, 1.0], (N, K))
    g = wide(rng, N, 128, 4 * P).astype(np.float32).reshape(N, 128, P, 4)
    g[:, :, e] = np.abs(g[:, :, e]) * np.sign(d["u"][0, :, None, :4].astype(np.float32))
    d["gr"] = times(g.reshape(N, 128, -1), np.repeat(k, 4, axis=1)[:, None])
    return d
def setup_inputs_ties(rng):
    d = plain(rng)
    x = f(rng, 128, 24).astype(np.float32).reshape(128, 6, 4)
    h = np.stack([rng.permutation(P) % 6 for r in range(N)])
    sign = rng.choice([-1.0, 1.0], (N, 1, P, 1))
    d["gr"] = times((np.moveaxis(x[:, h], 1, 0) * sign).reshape(N, 128, -1), 1)
    return d
def check_inputs(d):
    b = []
    for k, lo, hi in (("gr", -16, 24), ("u", -30, 30), ("w", -30, 30)):
        v = np.abs(d[k].astype(np.float32))
        if not (np.isfinite(v).all() and ((v == 0) | (v >= 2.0 ** lo) & (v <= 2.0 ** hi)).all()): b.append("a value of " + k)
    v = d["u"].astype(np.float32)
    if (v[:, :, 4:] != 0).any(): b.append("u has numbers behind its column 0")
    if (v != v[:1]).any(): b.append("u isn't the same on all ranks")
    return b
def size(ku, q):
    return np.abs(mx_ref.matmul(ku, q)[0])
def best(s):
    return np.sort(np.argsort(-s, kind="stable")[:K])
def merge(ku, a, b):
    i, j = np.intersect1d(a[0], b[0], return_indices=True)[1:]
    q = join(a[1], b[1])
    v = decode(q).reshape(128, 2 * K, 4)
    v[:, i] = v[:, i] + v[:, K + j]
    q = put(q, i, pick(mx_ref.quantize(np.ascontiguousarray(v.reshape(128, -1).astype(BF))), i))
    n = np.concatenate([a[0], b[0]])
    e = np.setdiff1d(np.arange(2 * K), K + j)
    e = e[np.argsort(n[e])]
    e = e[best(size(ku, q)[e])]
    return n[e], pick(q, e)
def reference(gr, u, w):
    ku, S = [mx_ref.quantize(np.ascontiguousarray(u[r])) for r in range(N)], []
    for r in range(N):
        q = mx_ref.quantize(np.ascontiguousarray(gr[r]))
        e = best(size(ku[r], q))
        S.append((e, pick(q, e)))
    for b in range(L):
        new = list(S)
        for r in range(N):
            p = r ^ (1 << b)
            if r < p: new[r] = new[p] = merge(ku[r], S[r], S[p])
        S = new
    oc, osc = np.zeros((N, 128, 4 * K), np.uint8), np.zeros((N, 16, K), np.uint8)
    nb, y = np.zeros((N, 1, K), np.float32), np.zeros((N, 128, O * K), np.float32)
    for r in range(N):
        oc[r], osc[r] = emit(S[r][1])
        nb[r, 0] = S[r][0]
        for o in range(O): y[r, :, o * K:o * K + K] = mx_ref.matmul(mx_ref.quantize(np.ascontiguousarray(cut(w[r], o))), S[r][1])
    return {"oc": oc, "osc": osc, "nb": nb, "y": y}

@@ -1,0 +1,427 @@
+from concourse.mybir import dt, AluOpType as OP, AxisListType, ActivationFunctionType as AF
+
+BIG = 1.0e29
+FLOOR = 2.0 ** -124
+BELOW = 1.0 - 2.0 ** -24
+MAGIC = 1.5 * 2.0 ** 27
+
+F32, B16, I32, U16, U8, MX = "float32", "bfloat16", "int32", "uint16", "uint8", "float8_e4m3fn_x4"
+SCRATCH = {}
+for _d, _names in (
+        (B16, "ut 16|grt 1024|wt 512|ones 520|zer 512|ur 512|zd 520|iot 256|hp 512|dgb 64|kr 64|neg1 64|xx0 576|xx 560"
+              "|pt 512|c0 256|c1 256|c2 256|c3 256|ht0 1024|t10 256|t11 256|t12 256|t40 256|t41 256|t42 256|m_nr 128|m_dx 128|m_dy 128"
+              "|m_gt 128|m_da 320|m_pa 256|m_mt 512|m_ht 512|nbz 192"),
+        (F32, "cst 16|mask 64|rst 64|m4 4|phi 4|plo 4|ph64 4|jc 4|sr0 256|sc0 8|ld0 128|ldz 128|d0 128|d1 128|rk0 8|nbs 64|ys 64|ytab 192"
+              "|m_c 16|m_r 8|m_sc 8|m_v 16|m_eq 128|m_eq2 128|m_g4 64|m_g5 64|m_vv 64|m_fa 4|m_fb 4|m_rw 64|m_sra 64|m_w 128|m_f 128|m_m 128|m_cc 128"),
+        (I32, "pi 8|bi 8|bj 8"),
+        (U16, "hl 4|lst0 8|lst1 8|lst2 12|lst3 8|bl0 4|bl1 4|bl2 2|bu 4|m_toff 4|m_fl 4")):
+    for _n in _names.split("|"):
+        SCRATCH[_n.split()[0]] = ("sbuf", [128, int(_n.split()[1])], _d)
+for _n, _w in (("u", 128), ("e", 512), ("g", 256), ("w", 128), ("n", 128), ("x0", 144), ("x", 140), ("p", 128), ("h0", 256), ("h", 128)):
+    SCRATCH["q" + _n] = ("sbuf", [128, _w], MX)
+    SCRATCH["s" + _n] = ("sbuf", [128, _w], U8)
+for _n, _w in [("z%d" % _b, 384) for _b in range(3)] + [("y3", 64)]:
+    SCRATCH[_n] = ("sbuf", [128, _w], MX)
+    SCRATCH["s" + _n] = ("sbuf", [128, _w], U8)
+SCRATCH["hc"] = ("sbuf", [128, 64], MX)
+SCRATCH["hs"] = ("sbuf", [128, 64], U8)
+SCRATCH["PE"] = ("psum", [128, 2048], F32)
+for _n in ("PR", "PC", "PL", "PS"):
+    SCRATCH[_n] = ("psum", [128, 512], F32)
+
+SEMAPHORES = (["kv", "ka", "kt", "kg", "sent", "hc", "hs", "hl"] + ["al%d" % b for b in range(3)] + ["ac%d" % b for b in range(3)]
+              + ["ld%d" % i for i in range(4)] + ["st%d" % i for i in range(8)])
+
+
+def make_flow(g, T):
+    eng = {"v": g.vector, "a": g.scalar, "t": g.tensor, "g": g, "s": g.sync}
+    own = {"v": "kv", "a": "ka", "t": "kt", "g": "kg"}
+    total, clock, ev, wr, rd, order = {}, {k: {} for k in eng}, {}, {}, {}, {}
+
+    def need(q, events):
+        for e in sorted(events, key=lambda e: -order.get(e, 0)):
+            sem, val = e
+            if clock[q].get(sem, 0) >= val:
+                continue
+            eng[q].wait_ge(T.sem[sem], val)
+            for s, v in ev.get(e, {}).items():
+                clock[q][s] = max(clock[q].get(s, 0), v)
+            clock[q][sem] = max(clock[q].get(sem, 0), val)
+
+    def deps(mine, reads, writes):
+        out = set()
+        for t in reads:
+            if t not in wr:
+                raise ValueError("nothing wrote " + t)
+            out.add(wr[t])
+        for t in writes:
+            if t in wr and wr[t][0] != mine:
+                out.add(wr[t])
+            for e in rd.get(t, ()):
+                if e[0] != mine:
+                    out.add(e)
+        return out
+
+    def note(q, e, reads, writes):
+        ev[e] = dict(clock[q])
+        ev[e][e[0]] = e[1]
+        order[e] = len(order) + 1
+        for t in reads:
+            rd.setdefault(t, []).append(e)
+        for t in writes:
+            wr[t] = e
+            rd[t] = []
+
+    def op(q, reads, writes, fn):
+        sem = own[q]
+        need(q, deps(sem, reads, writes))
+        total[sem] = total.get(sem, 0) + 1
+        fn(eng[q]).then_inc(T.sem[sem], 1)
+        note(q, (sem, total[sem]), reads, writes)
+
+    def dma(q, reads, writes, sem, out, in_):
+        need(q, deps(None, reads, writes))
+        eng[q].dma_start(out, in_).then_inc(T.sem[sem], 16)
+        total[sem] = total.get(sem, 0) + 16
+        note(q, (sem, total[sem]), reads, writes)
+
+    def arrives(tok, sem, val):
+        ev[(sem, val)] = {sem: val}
+        order[(sem, val)] = len(order) + 1
+        total[sem] = val
+        wr[tok] = (sem, val)
+        rd[tok] = []
+
+    def ready(q, reads):
+        need(q, deps(None, reads, []))
+
+    def finish():
+        need("g", list(total.items()))
+
+    return op, dma, arrives, ready, finish
+
+
+def rank_program(g, core, T, topo):
+    rank = T.rank_of(core)
+    sent = [0]
+    PARTNER, OWN = slice(128, 192), slice(192, 256)
+
+    def send(out, in_, dst, sem, away=None):
+        e = [x for x in topo.engines(core, dst) if away is None or x in topo.engines(core, away)]
+        rid, pid = topo.addr(dst, core)
+        g.remote_dma(out, in_, T.sem[sem], T.sem.sent, pid, rid, sum(1 << x for x in e))
+        sent[0] += len(e)
+
+    def helpers(r):
+        c0, far = T.cores[r], T.cores[r ^ 1]
+        hs = [c for c in topo.cores_of(c0) if c != c0 and topo.die(c) == topo.die(c0) and topo.may_write(c, far)]
+        return hs[0], hs[-1]
+
+    def bits(v):
+        return v.bitcast(dt.uint8)
+
+    if rank is None:
+        for r in range(len(T.cores)):
+            a, b = helpers(r)
+            if core not in (a, b):
+                continue
+            far = T.cores[r ^ 1]
+            n = len([x for x in topo.engines(T.cores[r], core) if x in topo.engines(T.cores[r], T.cores[r ^ 2])])
+            if core == b:
+                g.wait_ge(T.sem.hl, n)
+                send(T.bl0[:], T.hl[:], far, "al0")
+            if core == a:
+                g.wait_ge(T.sem.hc, n)
+                send(bits(T.z0[:, PARTNER]), bits(T.hc[:]), far, "ac0")
+            if core == b:
+                g.wait_ge(T.sem.hs, n)
+                send(T.sz0[:, PARTNER], T.hs[:], far, "ac0")
+            g.wait_ge(T.sem.sent, sent[0])
+        return
+
+    op, dma, arrives, ready, finish = make_flow(g, T)
+    X = AxisListType.X
+    pf, pm, nisa, okb, floor = [T.cst[:, i:i + 1] for i in range(5)]
+    nc, cnt, okc = [T.m_c[:, i:i + 1] for i in range(3)]
+    v, hc, mc, ph, cc = [T.m_v[:, i:i + 1] for i in range(5)]
+    rk, rkb, sel = [T.m_r[:, i:i + 1] for i in range(3)]
+    sc = T.m_sc[:, 0:1]
+
+    dma("s", [], ["gr0"], "ld1", T.grt[:, 0:512], T.gr[:, 0:512])
+    dma("a", [], ["ut"], "ld0", T.ut[:, 0:4], T.u[:, 0:4])
+    dma("a", [], ["gr1"], "ld2", T.grt[:, 512:1024], T.gr[:, 512:1024])
+    dma("s", [], ["wt"], "ld3", T.wt[:], T.w[:])
+
+    op("g", [], ["pi"], lambda e: e.iota(T.pi[:, 0:1], [[0, 1]], 0, 1))
+    op("v", [], ["ldz"], lambda e: e.memset(T.ldz[:], BELOW))
+    op("v", [], ["m4"], lambda e: e.memset(T.m4[:], MAGIC))
+    op("v", [], ["onesa"], lambda e: e.memset(T.ones[:, 0:128], 1.0))
+    op("v", [], ["onesb"], lambda e: e.memset(T.ones[:, 128:520], 1.0))
+    op("v", ["pi"], ["pf"], lambda e: e.tensor_copy(pf, T.pi[:, 0:1]))
+    op("v", [], ["floor"], lambda e: e.memset(floor, FLOOR))
+    op("v", [], ["xx0z"], lambda e: e.memset(T.xx0[:], 0.0))
+    op("v", ["m4", "pf"], ["phi"], lambda e: e.tensor_scalar(T.phi[:], T.m4[:], pf, MAGIC, OP.add, OP.subtract))
+    op("v", [], ["zer"], lambda e: e.memset(T.zer[:], 0.0))
+    op("v", ["phi", "pf"], ["plo"], lambda e: e.tensor_scalar(T.plo[:], T.phi[:], pf, -1.0, OP.subtract, OP.mult))
+    op("g", ["ldz"], ["ld0"], lambda e: e.affine_select(T.ld0[:], T.ldz[:], [[-1, 128]], OP.is_gt, 1.0, 0, 1))
+    op("g", ["onesa", "onesb"], ["zd"], lambda e: e.affine_select(T.zd[:, 0:516], T.ones[:, 0:516], [[-1, 516]], OP.is_equal, 0.0, 3, 4))
+    op("g", [], ["kr"], lambda e: e.iota(T.kr[:], [[0, 4], [1, 16]], 0, 0, allow_small_or_imprecise_dtypes=True))
+    op("g", [], ["hp"], lambda e: e.iota(T.hp[:], [[0, 8], [1, 16], [16, 4]], 0, 0, allow_small_or_imprecise_dtypes=True))
+    op("g", [], ["iot"], lambda e: e.iota(T.iot[:], [[1, 256]], 0, 0, allow_small_or_imprecise_dtypes=True))
+    op("g", [], ["t10"], lambda e: e.iota(T.t10[:], [[0, 256]], 64, 0, allow_small_or_imprecise_dtypes=True))
+    op("g", ["onesa"], ["dgb"], lambda e: e.affine_select(T.dgb[:], T.ones[:, 0:64], [[-1, 64]], OP.is_equal, 0.0, -64, 1))
+    for i, src, add in ((0, "phi", 0.0), (32, "phi", 128.0), (64, "plo", 0.0)):
+        op("a", [src, "xx0z"], ["xx0"], lambda e: e.activation(T.xx0[:, i:i + 16:5], T[src][:], AF.Copy, bias=add))
+    for t in range(4):
+        op("v", ["onesa", "ut"], ["ur"], lambda e: e.tensor_scalar(T.ur[:, t:512:4], T.ones[:, 0:128], T.ut[:, t:t + 1], None, OP.mult))
+    H = [slice(0, 128), slice(128, 256)]
+    op("v", ["gr0"], ["qg0"], lambda e: e.quantize_mx(T.qg[:, H[0]], T.sg[:, H[0]], T.grt[:, 0:512]))
+    op("v", ["ur"], ["qu"], lambda e: e.quantize_mx(T.qu[:], T.su[:], T.ur[:]))
+    op("v", ["gr1"], ["qg1"], lambda e: e.quantize_mx(T.qg[:, H[1]], T.sg[:, H[1]], T.grt[:, 512:1024]))
+    op("v", ["xx0"], ["qx0"], lambda e: e.quantize_mx(T.qx0[:], T.sx0[:], T.xx0[:]))
+
+    def unpacker(t):
+        op("v", ["zd"], ["qe"], lambda e: e.quantize_mx(T.qe[:, 128 * t:128 * t + 128], T.se[:, 128 * t:128 * t + 128], T.zd[:, 3 - t:515 - t]))
+
+    def zeros(b):
+        z, s = T["z%d" % b], T["sz%d" % b]
+        op("v", ["zer"], ["z%dm" % b], lambda e: e.quantize_mx(z[:, 256:384], s[:, 256:384], T.zer[:]))
+        op("v", ["zer"], ["z%dz" % b], lambda e: e.quantize_mx(z[:, 0:128], s[:, 0:128], T.zer[:]))
+
+    for h, P in ((0, "PC"), (1, "PS")):
+        op("t", ["qu", "qg%d" % h], [P], lambda e: e.matmul_mx(T[P][:, 0:128], T.qg[:, H[h]], T.sg[:, H[h]], T.qu[:], T.su[:], True, True))
+        op("t", ["qu", "qg%d" % h], ["PE%d" % h], lambda e: e.matmul_mx(T.PE[:, 512 * h:512 * h + 128], T.qu[:], T.su[:], T.qg[:, H[h]], T.sg[:, H[h]], True, True))
+        op("a", [P, "floor"], ["sc0%d" % h], lambda e: e.activation(T.sc0[:, h:h + 1], T[P][:, 0:1], AF.Abs, bias=floor))
+        op("a", ["PE%d" % h, "floor"], ["sr0%d" % h], lambda e: e.activation(T.sr0[:, H[h]], T.PE[:, 512 * h:512 * h + 128], AF.Abs, bias=floor))
+
+    def across(h):
+        op("v", ["sr0%d" % (1 - h), "sc0%d" % h], ["c%da" % h], lambda e: e.tensor_scalar(
+            T["c%d" % h][:, H[1 - h]], T.sr0[:, H[1 - h]], T.sc0[:, h:h + 1], None, OP.is_ge if h else OP.is_gt))
+
+    def passed(h):
+        op("v", ["ld0", "sc0%d" % h], ["d%d" % h], lambda e: e.tensor_scalar(T["d%d" % h][:], T.ld0[:], T.sc0[:, h:h + 1], None, OP.mult))
+
+    def within(h):
+        op("v", ["sr0%d" % h, "d%d" % h], ["c%db" % h], lambda e: e.tensor_tensor(T["c%d" % h][:, H[h]], T.sr0[:, H[h]], T["d%d" % h][:], OP.is_gt))
+
+    def total(h, k, i):
+        part = H[1 - h] if k == "a" else H[h]
+        op("a", ["c%d%s" % (h, k)], ["rk%d%s" % (h, k), "cx%d%s" % (h, k)], lambda e: e.activation(
+            T["c%d" % (h + 2)][:, part], T["c%d" % h][:, part], AF.Copy, accum_out=T.rk0[:, i:i + 1]))
+
+    def onehot(h):
+        op("v", ["hp", "rk%da" % h, "rk%db" % h], ["ht0%d" % h], lambda e: e.tensor_scalar(
+            T.ht0[:, 512 * h:512 * h + 512], T.hp[:], T.rk0[:, 2 * h:2 * h + 1], T.rk0[:, 2 * h + 1:2 * h + 2], OP.subtract, OP.is_equal))
+
+    op("v", ["pi"], ["pi15"], lambda e: e.tensor_scalar(T.pi[:, 1:2], T.pi[:, 0:1], 15, None, OP.bitwise_and))
+    unpacker(0)
+    passed(0)
+    op("v", ["pi15"], ["pm"], lambda e: e.tensor_copy(pm, T.pi[:, 1:2]))
+    op("v", ["kr"], ["rst"], lambda e: e.tensor_scalar(T.rst[:], T.kr[:], 0.5, None, OP.is_gt))
+    within(0)
+    passed(1)
+    across(0)
+    across(1)
+    within(1)
+    total(0, "b", 0)
+    total(0, "a", 1)
+    total(1, "a", 2)
+    total(1, "b", 3)
+    unpacker(1)
+    onehot(0)
+    op("v", ["kr", "pm"], ["mask"], lambda e: e.tensor_scalar(T.mask[:], T.kr[:], pm, None, OP.is_equal))
+    onehot(1)
+    for h in range(2):
+        op("v", ["ht0%d" % h], ["qh0%d" % h], lambda e: e.quantize_mx(T.qh0[:, H[h]], T.sh0[:, H[h]], T.ht0[:, 512 * h:512 * h + 512]))
+        for c in (8 * h, 16):
+            op("t", ["qh0%d" % h, "qx0"], ["PL"], lambda e: e.matmul_mx(
+                T.PL[:, 0:128], T.qh0[:, H[h]], T.sh0[:, H[h]], T.qx0[:, c:c + 128], T.sx0[:, c:c + 128], h == 0 and c == 0, h == 1 and c == 16))
+    zeros(0)
+    unpacker(2)
+    unpacker(3)
+    op("v", [], ["daz"], lambda e: e.memset(T.m_da[:, 64:320:80], 0.0))
+    op("v", ["PL"], ["lst0"], lambda e: e.tensor_copy(T.lst0[:, 0:4], T.PL[:, 0:4]))
+    op("v", [], ["neg1"], lambda e: e.memset(T.neg1[:], -1.0))
+    op("v", ["hp", "pm"], ["jc"], lambda e: e.tensor_scalar(T.jc[:], T.hp[:, 0:4], pm, None, OP.add))
+
+    def pick(b, into, at):
+        src, ssrc, w, frm = (("qg", "sg", slice(0, 256), ["qg0", "qg1"]) if b == 0 else
+                             ("z%d" % (b - 1), "sz%d" % (b - 1), slice(128, 320), ["z%d%s" % (b - 1, k) for k in "psom"]))
+        lst = "lst%d" % b
+        op("v", frm + [lst], [into + "o"], lambda e: e.tensor_copy(
+            T[into][:, at].bitcast(dt.uint32), T[src][:, w].bitcast(dt.uint32).indirect(T[lst][:, 0:4])))
+        op("a", frm + [lst], [into + "s"], lambda e: e.activation(T["s" + into][:, at], T[ssrc][:, w].indirect(T[lst][:, 0:4]), AF.Copy))
+
+    ha, hb = helpers(rank)
+    away = T.cores[rank ^ 2]
+    ready("g", ["lst0"])
+    send(T.hl[:], T.lst0[:, 0:4], hb, "hl", away)
+    pick(0, "z0", OWN)
+    ready("g", ["z0o"])
+    send(bits(T.hc[:]), bits(T.z0[:, OWN]), ha, "hc", away)
+    ready("g", ["z0s"])
+    send(T.hs[:], T.sz0[:, OWN], hb, "hs", away)
+
+    def big(b):
+        op("g", ["iot"], ["t4%d" % b], lambda e: e.affine_select(T["t4%d" % b][:], T.iot[:], [[0, 256]], OP.is_gt, BIG, -1, 0))
+
+    def own_tables(b, aw, awt):
+        z, s, zt = T["z%d" % b], T["sz%d" % b], ["z%d%s" % (b, k) for k in "osm"]
+        op("v", ["iot", awt, "t1%d" % b], ["t1%d" % b], lambda e: e.tensor_copy(T["t1%d" % b][:].indirect(aw), T.iot[:, 0:64]))
+        op("a", ["iot", awt], ["nra"], lambda e: e.activation(T.m_nr[:, 0:64], T.iot[:].indirect(aw), AF.Copy))
+        op("g", ["nra"], ["dxa"], lambda e: e.affine_select(T.m_dx[:, 0:64], T.m_nr[:, 0:64], [[-1, 64]], OP.is_equal, 0.0, 0, 1))
+        if b == 0:
+            big(0)
+        for t in range(4):
+            op("t", ["qe"] + zt, ["PE%d" % t], lambda e: e.matmul_mx(
+                T.PE[:, 512 * t:512 * t + 128], T.qe[:, 128 * t:128 * t + 128], T.se[:, 128 * t:128 * t + 128], z[:, 192:320], s[:, 192:320], True, True))
+            op("a", ["PE%d" % t, "daz"], ["da%d" % t], lambda e: e.activation(T.m_da[:, 80 * t:80 * t + 64], T.PE[:, 512 * t:512 * t + 64], AF.Copy))
+        op("t", ["qu"] + zt, ["PR"], lambda e: e.matmul_mx(T.PR[:, 0:128], T.qu[:], T.su[:], z[:, 192:320], s[:, 192:320], True, True))
+
+    own_tables(0, T.lst0[:, 0:4], "lst0")
+    op("v", ["pf"], ["nisa"], lambda e: e.tensor_scalar(nisa, pf, 63.5, -1.0, OP.is_lt, OP.mult))
+    op("v", ["pf"], ["okb"], lambda e: e.tensor_scalar(okb, pf, 63.5, 1.0, OP.is_lt, OP.add))
+    op("v", ["phi"], ["ph64"], lambda e: e.tensor_scalar(T.ph64[:], T.phi[:], 64.0, None, OP.add))
+    op("v", [], ["mtz"], lambda e: e.memset(T.m_mt[:, 256:512], 0.0))
+    op("v", [], ["xxz"], lambda e: e.memset(T.xx[:], 0.0))
+    zeros(1)
+    op("v", ["plo", "xxz"], ["xxl"], lambda e: e.tensor_copy(T.xx[:, 48:64:5], T.plo[:]))
+
+    for b in range(3):
+        nx = b + 1
+        z, sz = T["z%d" % b], T["sz%d" % b]
+        own, mrg, prt = ["z%do" % b, "z%ds" % b], "z%dm" % b, "z%dp" % b
+        t1, t4 = "t1%d" % b, "t4%d" % b
+        aw, awt = (T.lst0[:, 0:4], "lst0") if b == 0 else (T["lst%d" % b][:, 4:8], "lst%d" % b)
+        src = helpers(rank ^ 1)[0] if b == 0 else T.cores[rank ^ (1 << b)]
+        n = len(topo.engines(src, core))
+        arrives("bl%d" % b, "al%d" % b, n)
+        arrives(prt, "ac%d" % b, 2 * n)
+
+        if b == 2:
+            op("v", ["bl2"], ["bi"], lambda e: e.tensor_copy(T.bi[:, 0:2], T.bl2[:]))
+            op("v", ["bi"], ["bj0"], lambda e: e.tensor_scalar(T.bj[:, 0:2], T.bi[:, 0:2], 255, None, OP.bitwise_and))
+            op("v", ["bi"], ["bj1"], lambda e: e.tensor_scalar(T.bj[:, 2:4], T.bi[:, 0:2], 8, None, OP.logical_shift_right))
+            op("v", ["bj0", "bj1"], ["bu"], lambda e: e.tensor_copy(T.bu[:], T.bj[:, 0:4]))
+        bwt = "bl%d" % b if b < 2 else "bu"
+        bw = T[bwt][:]
+        op("v", [t1, bwt, "mask"], ["g4"], lambda e: e.tensor_tensor(T.m_g4[:], T[t1][:].indirect(bw), T.mask[:], OP.mult))
+        op("v", ["iot", bwt, "dgb"], ["dxb"], lambda e: e.tensor_tensor(T.m_dx[:, 64:128], T.iot[:].indirect(bw), T.dgb[:], OP.mult))
+        op("v", ["g4", "rst"], ["g5"], lambda e: e.tensor_tensor_scan(T.m_g5[:], T.rst[:], T.m_g4[:], 0.0, OP.mult, OP.add))
+        op("v", [t1, bwt, "dgb"], ["vv"], lambda e: e.tensor_tensor(T.m_vv[:], T[t1][:].indirect(bw), T.dgb[:], OP.mult))
+        op("v", ["g5"], ["toff"], lambda e: e.tensor_copy(T.m_toff[:], T.m_g5[:, 15:64:16]))
+        op("v", ["g5"], ["fa"], lambda e: e.tensor_scalar(T.m_fa[:], T.m_g5[:, 15:64:16], 63.5, 64.0, OP.is_lt, OP.mult))
+        op("v", ["vv"], ["v"], lambda e: e.tensor_reduce(v, T.m_vv[:], X, OP.add))
+        op("a", ["iot", bwt], ["nrb"], lambda e: e.activation(T.m_nr[:, 64:128], T.iot[:].indirect(bw), AF.Copy))
+        op("a", ["dxa", "dxb"], ["nc", "dy"], lambda e: e.activation(T.m_dy[:], T.m_dx[:], AF.Copy, accum_out=nc))
+        if b < 2:
+            op("g", [], ["t1%d" % nx], lambda e: e.iota(T["t1%d" % nx][:], [[0, 256]], 64, 0, allow_small_or_imprecise_dtypes=True))
+            big(nx)
+        if b == 0:
+            op("g", [], ["ptz"], lambda e: e.iota(T.pt[:], [[0, 512]], 0, 0, allow_small_or_imprecise_dtypes=True))
+        for t in range(4):
+            pa, da = T.m_pa[:, 64 * t:64 * t + 64], T.m_da[:, 80 * t:80 * t + 65].indirect(T.m_toff[:])
+            if t < 2:
+                op("v", ["da%d" % t, "toff"], ["pa%d" % t], lambda e: e.tensor_copy(pa, da))
+            else:
+                op("a", ["da%d" % t, "toff"], ["pa%d" % t], lambda e: e.activation(pa, da, AF.Copy))
+        op("v", ["v"], ["hc"], lambda e: e.tensor_scalar(hc, v, 63.5, None, OP.is_gt))
+        op("v", ["v"], ["mc"], lambda e: e.tensor_scalar(mc, v, 63.5, None, OP.is_lt))
+        op("a", ["PR", "floor"], ["rw"], lambda e: e.activation(T.m_rw[:], T.PR[:, 0:64], AF.Abs, bias=floor))
+        op("a", ["nra", "nrb", "nc"], ["eq"], lambda e: e.activation(T.m_eq[:], T.m_nr[:], AF.Abs, bias=nc, scale=-1.0))
+        op("a", ["eq"], ["cnt", "eq2"], lambda e: e.activation(T.m_eq2[:], T.m_eq[:], AF.Relu, bias=1.0, scale=-1.0, accum_out=cnt))
+
+        for t in range(4):
+            op("t", ["qe", prt] + own, ["PE%d" % t], lambda e: e.matmul_mx(
+                T.PE[:, 512 * t:512 * t + 128], T.qe[:, 128 * t:128 * t + 128], T.se[:, 128 * t:128 * t + 128], z[:, 128:256], sz[:, 128:256], True, True))
+        op("t", ["qu", "z%dz" % b, prt], ["PL"], lambda e: e.matmul_mx(T.PL[:, 0:128], z[:, 64:192], sz[:, 64:192], T.qu[:], T.su[:], True, True))
+        op("t", ["qu", prt] + own, ["PR"], lambda e: e.matmul_mx(T.PR[:, 0:128], T.qu[:], T.su[:], z[:, 128:256], sz[:, 128:256], True, True))
+        for t in (0, 2, 1, 3):
+            op("v", ["PE%d" % t, "pa%d" % t], ["mt%d" % t], lambda e: e.tensor_tensor(
+                T.m_mt[:, t:256:4], T.PE[:, 512 * t:512 * t + 64], T.m_pa[:, 64 * t:64 * t + 64], OP.add))
+        op("v", ["nra", "nrb", "nc"], ["f"], lambda e: e.tensor_scalar(T.m_f[:], T.m_nr[:], nc, BELOW, OP.is_ge, OP.max))
+        op("v", ["fa", "jc"], ["fb"], lambda e: e.tensor_tensor(T.m_fb[:], T.m_fa[:], T.jc[:], OP.add))
+        op("v", ["mt0", "mt1", "mt2", "mt3", "mtz"], [mrg], lambda e: e.quantize_mx(z[:, 256:384], sz[:, 256:384], T.m_mt[:]))
+        op("t", ["qu", mrg] + own, ["PC"], lambda e: e.matmul_mx(T.PC[:, 0:128], z[:, 192:320], sz[:, 192:320], T.qu[:], T.su[:], True, True))
+        op("t", ["qu", mrg] + own, ["PS"], lambda e: e.matmul_mx(T.PS[:, 0:128], T.qu[:], T.su[:], z[:, 192:320], sz[:, 192:320], True, True))
+        op("v", ["PL", "hc"], ["cc"], lambda e: e.tensor_scalar(cc, T.PL[:, 0:1], hc, FLOOR, OP.mult, OP.add))
+        if b < 2:
+            op("v", ["m4", "nc", "xxz"], ["xxn"], lambda e: e.tensor_scalar(T.xx[:, 16:32:5], T.m4[:], nc, MAGIC, OP.add, OP.subtract))
+        else:
+            op("v", ["nra", "nrb", "nc"], ["gt"], lambda e: e.tensor_scalar(T.m_gt[:], T.m_nr[:], nc, 1000.0, OP.is_le, OP.mult))
+        op("v", ["v"], ["ph"], lambda e: e.tensor_scalar(ph, v, 63.5, -128.0, OP.is_gt, OP.mult))
+        op("v", [t4, "neg1", bwt], [t4], lambda e: e.tensor_copy(T[t4][:].indirect(bw), T.neg1[:]))
+        op("v", ["ph64", "ph", "xxz"], ["xxh"], lambda e: e.tensor_scalar(T.xx[:, 0:16:5], T.ph64[:], ph, None, OP.add))
+        if b < 2:
+            op("v", ["xxn", "nc"], ["xxm"], lambda e: e.tensor_scalar(T.xx[:, 64:80:5], T.xx[:, 16:32:5], nc, -1.0, OP.subtract, OP.mult))
+        op("v", ["fb"], ["fl"], lambda e: e.tensor_copy(T.m_fl[:], T.m_fb[:]))
+        op("v", [t4, "rw", awt], ["sra"], lambda e: e.tensor_tensor(T.m_sra[:], T[t4][:].indirect(aw), T.m_rw[:], OP.min))
+        op("a", ["cnt", "nisa", "okb"], ["ok"], lambda e: e.activation(okc, cnt, AF.Identity, bias=okb, scale=nisa))
+        op("a", ["PR", "floor"], ["wp"], lambda e: e.activation(T.m_w[:, 0:64], T.PR[:, 0:64], AF.Abs, bias=floor))
+
+        op("a", ["PC", "mc", "cc"], ["sc"], lambda e: e.activation(sc, T.PC[:, 0:1], AF.Abs, bias=cc, scale=mc))
+        op("a", ["PS", "floor"], ["wm"], lambda e: e.activation(T.m_w[:, 64:128], T.PS[:, 64:128], AF.Abs, bias=floor))
+        if b == 1:
+            for i in (0, 48):
+                op("a", ["xxn", "xxm"], ["xxp"], lambda e: e.activation(T.xx[:, i + 32:i + 38:5], T.xx[:, i + 16:i + 22:5], AF.Copy))
+                op("a", ["xxn", "xxm"], ["xxp"], lambda e: e.activation(T.xx[:, i + 34:i + 40:5], T.xx[:, i + 16:i + 22:5], AF.Copy, scale=256.0))
+        for k, i in (("m0", 0), ("m1", 64)):
+            op("v", ["f", "sc", "ok"], [k], lambda e: e.tensor_scalar(T.m_m[:, i:i + 64], T.m_f[:, i:i + 64], sc, okc, OP.mult, OP.mult))
+        op("v", ["sra", "m0"], ["cca"], lambda e: e.tensor_tensor(T.m_cc[:, 0:64], T.m_sra[:], T.m_m[:, 0:64], OP.is_gt))
+        op("v", ["wp", "wm", "fl", "m1"], ["ccb"], lambda e: e.tensor_tensor(T.m_cc[:, 64:128], T.m_w[:].indirect(T.m_fl[:]), T.m_m[:, 64:128], OP.is_gt))
+
+        def places():
+            op("v", ["xxl", "xxh", "xxn", "xxm"] + (["xxp"] if b == 1 else []), ["qx"], lambda e: e.quantize_mx(T.qx[:], T.sx[:], T.xx[:]))
+
+        if b < 2:
+            op("v", ["cca"], ["rka"], lambda e: e.tensor_reduce(rk, T.m_cc[:, 0:64], X, OP.add))
+            op("v", ["ccb"], ["rkb"], lambda e: e.tensor_reduce(rkb, T.m_cc[:, 64:128], X, OP.add))
+            places()
+            op("v", ["hp", "rka", "rkb"], ["ht"], lambda e: e.tensor_scalar(T.m_ht[:], T.hp[:], rk, rkb, OP.subtract, OP.is_equal))
+        else:
+            op("v", ["cca", "ccb"], ["rka"], lambda e: e.tensor_reduce(rk, T.m_cc[:], X, OP.add))
+            op("t", ["qw", mrg, prt] + own, ["PE0"], lambda e: e.matmul_mx(T.PE[:, 0:192], T.qw[:], T.sw[:], z[:, 128:320], sz[:, 128:320], True, True))
+            op("a", ["PE0"], ["yt"], lambda e: e.activation(T.ytab[:], T.PE[:, 0:192], AF.Copy))
+            op("a", ["nra", "nrb"], ["nbz0"], lambda e: e.activation(T.nbz[:, 0:64], T.m_nr[:, 64:128], AF.Copy))
+            op("a", ["nra", "nrb"], ["nbz1"], lambda e: e.activation(T.nbz[:, 64:192], T.m_nr[:], AF.Copy))
+            op("v", ["gt", "rka", "ptz"], ["pt"], lambda e: e.tensor_scalar(T.pt[:, 0:512:4], T.m_gt[:], rk, 63.5, OP.add, OP.is_lt))
+            op("v", ["rka"], ["sel"], lambda e: e.tensor_scalar(sel, rk, 63.5, None, OP.is_lt))
+            op("v", ["pt"], ["qp"], lambda e: e.quantize_mx(T.qp[:], T.sp[:], T.pt[:]))
+            places()
+            op("t", ["qp", "qn"], ["PC"], lambda e: e.matmul_mx(T.PC[:, 0:128], T.qp[:], T.sp[:], T.qn[:], T.sn[:], True, True))
+            op("v", ["hp", "PC", "sel"], ["ht"], lambda e: e.tensor_scalar(T.m_ht[:], T.hp[:], T.PC[:, 0:1], sel, OP.is_equal, OP.mult))
+        op("v", ["ht"], ["qh"], lambda e: e.quantize_mx(T.qh[:], T.sh[:], T.m_ht[:]))
+        for c in (0, 12):
+            op("t", ["qh", "qx"], ["PL"], lambda e: e.matmul_mx(T.PL[:, 0:128], T.qh[:], T.sh[:], T.qx[:, c:c + 128], T.sx[:, c:c + 128], c == 0, c == 12))
+        if b == 0:
+            zeros(2)
+        if b == 1:
+            op("v", ["onesa", "onesb"], ["qn"], lambda e: e.quantize_mx(T.qn[:], T.sn[:], T.ones[:, 0:512]))
+            op("v", ["wt"], ["qw"], lambda e: e.quantize_mx(T.qw[:], T.sw[:], T.wt[:]))
+        lst = "lst%d" % nx
+        k = (8, 10, 4)[b]
+        op("v", ["PL"], [lst], lambda e: e.tensor_copy(T[lst][:, 0:k], T.PL[:, 0:k]))
+        if b < 2:
+            to = T.cores[rank ^ (1 << nx)]
+            ready("g", [lst])
+            send(T["bl%d" % nx][:], T[lst][:, 4:8] if b == 0 else T[lst][:, 8:10], to, "al%d" % nx)
+            o = "z%d" % nx
+            pick(nx, o, OWN)
+            ready("g", [o + "o"])
+            send(bits(T[o][:, PARTNER]), bits(T[o][:, OWN]), to, "ac%d" % nx)
+            ready("g", [o + "s"])
+            send(T["s" + o][:, PARTNER], T["s" + o][:, OWN], to, "ac%d" % nx)
+            own_tables(nx, T[lst][:, 4:8], lst)
+
+    pick(3, "y3", slice(0, 64))
+    dma("s", ["y3o"], [], "st0", T.oc[:], bits(T.y3[:]))
+    op("v", ["yt", "lst3"], ["ys"], lambda e: e.tensor_copy(T.ys[:], T.ytab[:].indirect(T.lst3[:, 0:4])))
+    op("a", ["nbz0", "nbz1", "lst3"], ["nbs"], lambda e: e.activation(T.nbs[:], T.nbz[:].indirect(T.lst3[:, 0:4]), AF.Copy))
+    dma("a", ["y3s"], [], "st1", T.osc[0:4, :], T.sy3[0:4, :])
+    dma("s", ["ys"], [], "st6", T.y[:], T.ys[:])
+    dma("a", ["y3s"], [], "st2", T.osc[4:8, :], T.sy3[32:36, :])
+    dma("a", ["y3s"], [], "st3", T.osc[8:12, :], T.sy3[64:68, :])
+    dma("s", ["nbs"], [], "st5", T.nb[:], T.nbs[0:1, :])
+    dma("a", ["y3s"], [], "st4", T.osc[12:16, :], T.sy3[96:100, :])
+    finish()
+    g.wait_ge(T.sem.sent, sent[0])

@@ -1,6 +1,7 @@
 from concourse.mybir import dt, AluOpType as OP, AxisListType, ActivationFunctionType as AF
 
-BIG = 1.0e29
+BIG = 1000.0
+HUGE = 2.0 ** 90
 FLOOR = 2.0 ** -124
 BELOW = 1.0 - 2.0 ** -24
 MAGIC = 1.5 * 2.0 ** 27
@@ -8,19 +9,20 @@ MAGIC = 1.5 * 2.0 ** 27
 F32, B16, I32, U16, U8, MX = "float32", "bfloat16", "int32", "uint16", "uint8", "float8_e4m3fn_x4"
 SCRATCH = {}
 for _d, _names in (
-        (B16, "ut 16|grt 1024|wt 512|ones 520|zer 512|ur 512|zd 520|iot 256|hp 512|dgb 64|kr 64|neg1 64|xx0 576|xx 560"
-              "|pt 512|c0 256|c1 256|c2 256|c3 256|ht0 1024|t10 256|t11 256|t12 256|t40 256|t41 256|t42 256|m_nr 128|m_dx 128|m_dy 128"
-              "|m_gt 128|m_da 320|m_pa 256|m_mt 512|m_ht 512|nbz 192"),
-        (F32, "cst 16|mask 64|rst 64|m4 4|phi 4|plo 4|ph64 4|jc 4|sr0 256|sc0 8|ld0 128|ldz 128|d0 128|d1 128|rk0 8|nbs 64|ys 64|ytab 192"
-              "|m_c 16|m_r 8|m_sc 8|m_v 16|m_eq 128|m_eq2 128|m_g4 64|m_g5 64|m_vv 64|m_fa 4|m_fb 4|m_rw 64|m_sra 64|m_w 128|m_f 128|m_m 128|m_cc 128"),
+        (B16, "ut 16|grt 1024|wt 512|ones 616|pat 32|zer 512|ur 512|zd 520|iot 256|hp 512|kr 64|dgb 64|xx 560"
+              "|pt 512|c0 256|c1 256|c2 256|c3 256|ht0 1024|m_nr 192|m_dx 128|m_dy 192"
+              "|m_gt 128|m_da 576|m_dn 1024|m_pa 256|m_mt 512|m_ht 512"),
+        (F32, "cst 16|mask 64|rst 64|m4 4|n4 4|phi 4|plo 4|ph128 4|jc 4|sr0 256|sc0 8|ld0 128|ldz 128|d0 128|d1 128|rk0 8"
+              "|nbs 64|ys 64|ytab 192|t10 256|t11 256|t12 256|m_c 16|m_r 8|m_sc 8|m_v 16|m_eq 64|m_eq2 64|m_g4 64|m_g5 64|m_fa 4|m_fb 4"
+              "|m_vv 72|m_rw 384|m_w 128|m_f 128|m_m 128|m_cc 136"),
         (I32, "pi 8|bi 8|bj 8"),
-        (U16, "hl 4|lst0 8|lst1 8|lst2 12|lst3 8|bl0 4|bl1 4|bl2 2|bu 4|m_toff 4|m_fl 4")):
+        (U16, "hl 2|lst0 8|lst1 8|lst2 8|lst3 8|bl0 2|bl1 4|bl2 4|bu 4|m_toff 4|m_fl 4")):
     for _n in _names.split("|"):
         SCRATCH[_n.split()[0]] = ("sbuf", [128, int(_n.split()[1])], _d)
 for _n, _w in (("u", 128), ("e", 512), ("g", 256), ("w", 128), ("n", 128), ("x0", 144), ("x", 140), ("p", 128), ("h0", 256), ("h", 128)):
     SCRATCH["q" + _n] = ("sbuf", [128, _w], MX)
     SCRATCH["s" + _n] = ("sbuf", [128, _w], U8)
-for _n, _w in [("z%d" % _b, 384) for _b in range(3)] + [("y3", 64)]:
+for _n, _w in [("z%d" % _b, 320) for _b in range(3)] + [("y3", 64)]:
     SCRATCH[_n] = ("sbuf", [128, _w], MX)
     SCRATCH["s" + _n] = ("sbuf", [128, _w], U8)
 SCRATCH["hc"] = ("sbuf", [128, 64], MX)
@@ -29,85 +31,123 @@ SCRATCH["PE"] = ("psum", [128, 2048], F32)
 for _n in ("PR", "PC", "PL", "PS"):
     SCRATCH[_n] = ("psum", [128, 512], F32)
 
-SEMAPHORES = (["kv", "ka", "kt", "kg", "sent", "hc", "hs", "hl"] + ["al%d" % b for b in range(3)] + ["ac%d" % b for b in range(3)]
-              + ["ld%d" % i for i in range(4)] + ["st%d" % i for i in range(8)])
+SEMAPHORES = (["kv", "ka", "kt", "kg", "sent", "hc", "hs", "hl", "st"] + ["al%d" % b for b in range(3)] + ["ac%d" % b for b in range(3)]
+              + ["ld%d" % i for i in range(4)])
+
+ORDER = {
+    "v": "floor m4 pat0 ldz pat2 pf onesa pat3 pat1 phi ph128 ur0 ur1 ur2 ur3 plo qu qg0 onesb qg1 qx0 d0 wi0 d1 ac0 ac1 wi1 twi1 ht0 ht1 qh0 qh1 "
+         "qe0 qe1 lst0 z0o qe2 qe3 pi15 off pm vvc jc mtz n4 huge xxz t1.0 rst mask zer xxl "
+         "bi bj0 bj1 bu vv.0 pa0.0 g4.0 mt1.0 v.0 dxb.0 g5.0 mt2.0 mt0.0 mt3.0 mc.0 hc.0 fa.0 qm.0 cc.0 strike.0 fb.0 ga.0 f.0 fl.0 wa.0 "
+         "m1.0 cca.0 ccb.0 xxn.0 rka.0 rkb.0 xxh.0 xxm.0 ht.0 qx.0 qh.0 zz1 daz cut lst1 z1o t1.1 da2.1 da3.1 "
+         "g4.1 dxb.1 g5.1 vv.1 toff.1 fa.1 v.1 pa0.1 pa1.1 mt0.1 hc.1 mt2.1 mt1.1 mt3.1 mc.1 fb.1 qm.1 cc.1 strike.1 ga.1 xxn.1 f.1 fl.1 wa.1 "
+         "m1.1 xxm.1 cca.1 ccb.1 rka.1 rkb.1 xxh.1 ht.1 qx.1 qh.1 zz2 qn lst2 z2o t1.2 da2.2 da3.2 qw "
+         "g4.2 dxb.2 g5.2 vv.2 toff.2 fa.2 v.2 pa0.2 pa1.2 mt0.2 hc.2 mt2.2 mt1.2 mt3.2 mc.2 fb.2 qm.2 cc.2 strike.2 ga.2 f.2 fl.2 wa.2 "
+         "m1.2 cca.2 ccb.2 rka.2 gt rkb.2 pt xxh.2 sel qp qx.2 ht.2 qh.2 lst3 y3o ys nbs",
+    "a": "gr1 xa64 xa0 xa32 sc0 sr0 sc1 sr1 twi0 tac0 tac1 z0s "
+         "nra.0 da0.0 da1.0 da2.0 da3.0 nca.0 pa1.0 pa2.0 pa3.0 nrb.0 eq.0 nc.0 wp.0 eq2.0 sc.0 wm.0 z1s "
+         "nra.1 da0.1 da1.1 rw.1 nrb.1 nca.1 pa2.1 pa3.1 nc.1 eq.1 wp.1 eq2.1 sc.1 wm.1 z2s "
+         "nra.2 da0.2 da1.2 rw.2 nrb.2 nca.2 pa2.2 pa3.2 nc.2 eq.2 wp.2 eq2.2 sc.2 wm.2 nrc yt y3s osc0 osc1 osc2 osc3",
+    "t": "col0 row0 col1 row1 ls0_0 ls0_16 ls1_8 ls1_16 "
+         "uo0.0 uo1.0 uo2.0 uo3.0 up0.0 up1.0 up2.0 up3.0 cp.0 rp.0 cm.0 rm.0 ls0.0 ls12.0 "
+         "uo2.1 uo0.1 uo1.1 uo3.1 ro.1 up0.1 up1.1 up2.1 up3.1 cp.1 rp.1 cm.1 rm.1 ls0.1 ls12.1 "
+         "uo2.2 uo0.2 uo1.2 uo3.2 ro.2 up0.2 up1.2 up2.2 up3.2 cp.2 rp.2 cm.2 rm.2 ymm pos ls0.2 ls12.2",
+    "g": "pi ld0 hp zd iot sl0 sc_0 ss0 tz0 kr dxa.0 dgb rwz tz1 tz2 sl1 sc_1 ss1 dxa.1 ptz sl2 sc_2 ss2 dxa.2",
+    "s": "ut gr0 wt oc y nb",
+}
 
 
 def make_flow(g, T):
     eng = {"v": g.vector, "a": g.scalar, "t": g.tensor, "g": g, "s": g.sync}
     own = {"v": "kv", "a": "ka", "t": "kt", "g": "kg"}
-    total, clock, ev, wr, rd, order = {}, {k: {} for k in eng}, {}, {}, {}, {}
+    calls, wr, rd = {}, {}, {}
 
-    def need(q, events):
-        for e in sorted(events, key=lambda e: -order.get(e, 0)):
-            sem, val = e
-            if clock[q].get(sem, 0) >= val:
-                continue
-            eng[q].wait_ge(T.sem[sem], val)
-            for s, v in ev.get(e, {}).items():
-                clock[q][s] = max(clock[q].get(s, 0), v)
-            clock[q][sem] = max(clock[q].get(sem, 0), val)
-
-    def deps(mine, reads, writes):
-        out = set()
+    def note(name, q, kind, reads, writes, fn, args, kw):
+        if name in calls:
+            raise ValueError("twice " + name)
+        raw, other = set(), set()
         for t in reads:
-            if t not in wr:
-                raise ValueError("nothing wrote " + t)
-            out.add(wr[t])
+            raw.add(wr[t])
         for t in writes:
-            if t in wr and wr[t][0] != mine:
-                out.add(wr[t])
-            for e in rd.get(t, ()):
-                if e[0] != mine:
-                    out.add(e)
-        return out
-
-    def note(q, e, reads, writes):
-        ev[e] = dict(clock[q])
-        ev[e][e[0]] = e[1]
-        order[e] = len(order) + 1
+            if t in wr:
+                other.add(wr[t])
+            other.update(rd.get(t, ()))
         for t in reads:
-            rd.setdefault(t, []).append(e)
+            rd.setdefault(t, []).append(name)
         for t in writes:
-            wr[t] = e
+            wr[t] = name
             rd[t] = []
+        other.discard(name)
+        calls[name] = (q, kind, raw, other, fn, args, kw)
 
-    def op(q, reads, writes, fn):
-        sem = own[q]
-        need(q, deps(sem, reads, writes))
-        total[sem] = total.get(sem, 0) + 1
-        fn(eng[q]).then_inc(T.sem[sem], 1)
-        note(q, (sem, total[sem]), reads, writes)
+    def op(name, q, reads, writes, fn, *args, **kw):
+        note(name, q, "op", reads, writes, fn, args, kw)
 
-    def dma(q, reads, writes, sem, out, in_):
-        need(q, deps(None, reads, writes))
-        eng[q].dma_start(out, in_).then_inc(T.sem[sem], 16)
-        total[sem] = total.get(sem, 0) + 16
-        note(q, (sem, total[sem]), reads, writes)
+    def dma(name, q, reads, writes, sem, out, in_):
+        note(name, q, "dma", reads, writes, sem, (out, in_), {})
 
-    def arrives(tok, sem, val):
-        ev[(sem, val)] = {sem: val}
-        order[(sem, val)] = len(order) + 1
-        total[sem] = val
-        wr[tok] = (sem, val)
-        rd[tok] = []
+    def remote(name, reads, fn, *args):
+        note(name, "g", "remote", reads, [], fn, args, {})
 
-    def ready(q, reads):
-        need(q, deps(None, reads, []))
+    def arrives(name, sem, val):
+        note(name, None, "arrives", [], [name], sem, val, {})
 
-    def finish():
-        need("g", list(total.items()))
+    def issue():
+        queue = {q: ORDER[q].split() for q in eng}
+        for q in eng:
+            if sorted(queue[q]) != sorted(n for n in calls if calls[n][0] == q):
+                raise ValueError("the order of queue " + q)
+        total, clock, event, known, age = {}, {k: {} for k in eng}, {}, {}, {}
+        for n, c in calls.items():
+            if c[1] == "arrives":
+                event[n] = (c[4], c[5])
+                known[n] = {c[4]: c[5]}
+                age[n] = 0
+                total[c[4]] = c[5]
 
-    return op, dma, arrives, ready, finish
+        def need(q, names):
+            for n in sorted(names, key=lambda n: (-age[n], n)):
+                sem, val = event[n]
+                if clock[q].get(sem, 0) >= val:
+                    continue
+                eng[q].wait_ge(T.sem[sem], val)
+                for s, v in known[n].items():
+                    clock[q][s] = max(clock[q].get(s, 0), v)
+
+        while any(queue.values()):
+            moved = False
+            for q in eng:
+                while queue[q] and all(d in age for d in calls[queue[q][0]][2] | calls[queue[q][0]][3]):
+                    n = queue[q].pop(0)
+                    kind, raw, other, fn, args, kw = calls[n][1:]
+                    moved = True
+                    age[n] = len(age) + 1
+                    need(q, raw | {d for d in other if kind != "op" or calls[d][0] != q or calls[d][1] != "op"})
+                    if kind == "remote":
+                        fn(*args)
+                        continue
+                    sem, step = (own[q], 1) if kind == "op" else (fn, 16)
+                    (fn(*args, **kw) if kind == "op" else eng[q].dma_start(*args)).then_inc(T.sem[sem], step)
+                    total[sem] = total.get(sem, 0) + step
+                    event[n] = (sem, total[sem])
+                    known[n] = dict(clock[q])
+                    known[n][sem] = total[sem]
+            if not moved:
+                raise ValueError("the queues wait for one another")
+        return [(sem, val) for sem, val in total.items() if clock["g"].get(sem, 0) < val]
+
+    return op, dma, remote, arrives, issue
 
 
 def rank_program(g, core, T, topo):
     rank = T.rank_of(core)
     sent = [0]
-    PARTNER, OWN = slice(128, 192), slice(192, 256)
+    OWN, PARTNER = slice(64, 128), slice(128, 192)
+
+    def engines(src, dst, away=None):
+        return [x for x in topo.engines(src, dst) if away is None or x in topo.engines(src, away)]
 
     def send(out, in_, dst, sem, away=None):
-        e = [x for x in topo.engines(core, dst) if away is None or x in topo.engines(core, away)]
+        e = engines(core, dst, away)
         rid, pid = topo.addr(dst, core)
         g.remote_dma(out, in_, T.sem[sem], T.sem.sent, pid, rid, sum(1 << x for x in e))
         sent[0] += len(e)
@@ -126,7 +166,7 @@ def rank_program(g, core, T, topo):
             if core not in (a, b):
                 continue
             far = T.cores[r ^ 1]
-            n = len([x for x in topo.engines(T.cores[r], core) if x in topo.engines(T.cores[r], T.cores[r ^ 2])])
+            n = len(engines(T.cores[r], core, T.cores[r ^ 2]))
             if core == b:
                 g.wait_ge(T.sem.hl, n)
                 send(T.bl0[:], T.hl[:], far, "al0")
@@ -139,289 +179,253 @@ def rank_program(g, core, T, topo):
             g.wait_ge(T.sem.sent, sent[0])
         return
 
-    op, dma, arrives, ready, finish = make_flow(g, T)
+    op, dma, remote, arrives, issue = make_flow(g, T)
+    V, A, PE = g.vector, g.scalar, g.tensor
     X = AxisListType.X
-    pf, pm, nisa, okb, floor = [T.cst[:, i:i + 1] for i in range(5)]
-    nc, cnt, okc = [T.m_c[:, i:i + 1] for i in range(3)]
-    v, hc, mc, ph, cc = [T.m_v[:, i:i + 1] for i in range(5)]
+    loose = {"allow_small_or_imprecise_dtypes": True}
+    pf, pm, off, huge, floor = [T.cst[:, i:i + 1] for i in range(5)]
+    nc, nca, hit = [T.m_c[:, i:i + 1] for i in range(3)]
+    hc, mc, cc, v = [T.m_v[:, i:i + 1] for i in range(4)]
     rk, rkb, sel = [T.m_r[:, i:i + 1] for i in range(3)]
     sc = T.m_sc[:, 0:1]
 
-    dma("s", [], ["gr0"], "ld1", T.grt[:, 0:512], T.gr[:, 0:512])
-    dma("a", [], ["ut"], "ld0", T.ut[:, 0:4], T.u[:, 0:4])
-    dma("a", [], ["gr1"], "ld2", T.grt[:, 512:1024], T.gr[:, 512:1024])
-    dma("s", [], ["wt"], "ld3", T.wt[:], T.w[:])
+    def mm(name, reads, bank, out, left, a, right, b, n=128, start=True, stop=True):
+        sl, sr = ["s" + (x[1:] if x[0] == "q" else x) for x in (left, right)]
+        op(name, "t", reads, [bank], PE.matmul_mx, out, T[left][:, a:a + 128], T[sl][:, a:a + 128], T[right][:, b:b + n], T[sr][:, b:b + n], start, stop)
 
-    op("g", [], ["pi"], lambda e: e.iota(T.pi[:, 0:1], [[0, 1]], 0, 1))
-    op("v", [], ["ldz"], lambda e: e.memset(T.ldz[:], BELOW))
-    op("v", [], ["m4"], lambda e: e.memset(T.m4[:], MAGIC))
-    op("v", [], ["onesa"], lambda e: e.memset(T.ones[:, 0:128], 1.0))
-    op("v", [], ["onesb"], lambda e: e.memset(T.ones[:, 128:520], 1.0))
-    op("v", ["pi"], ["pf"], lambda e: e.tensor_copy(pf, T.pi[:, 0:1]))
-    op("v", [], ["floor"], lambda e: e.memset(floor, FLOOR))
-    op("v", [], ["xx0z"], lambda e: e.memset(T.xx0[:], 0.0))
-    op("v", ["m4", "pf"], ["phi"], lambda e: e.tensor_scalar(T.phi[:], T.m4[:], pf, MAGIC, OP.add, OP.subtract))
-    op("v", [], ["zer"], lambda e: e.memset(T.zer[:], 0.0))
-    op("v", ["phi", "pf"], ["plo"], lambda e: e.tensor_scalar(T.plo[:], T.phi[:], pf, -1.0, OP.subtract, OP.mult))
-    op("g", ["ldz"], ["ld0"], lambda e: e.affine_select(T.ld0[:], T.ldz[:], [[-1, 128]], OP.is_gt, 1.0, 0, 1))
-    op("g", ["onesa", "onesb"], ["zd"], lambda e: e.affine_select(T.zd[:, 0:516], T.ones[:, 0:516], [[-1, 516]], OP.is_equal, 0.0, 3, 4))
-    op("g", [], ["kr"], lambda e: e.iota(T.kr[:], [[0, 4], [1, 16]], 0, 0, allow_small_or_imprecise_dtypes=True))
-    op("g", [], ["hp"], lambda e: e.iota(T.hp[:], [[0, 8], [1, 16], [16, 4]], 0, 0, allow_small_or_imprecise_dtypes=True))
-    op("g", [], ["iot"], lambda e: e.iota(T.iot[:], [[1, 256]], 0, 0, allow_small_or_imprecise_dtypes=True))
-    op("g", [], ["t10"], lambda e: e.iota(T.t10[:], [[0, 256]], 64, 0, allow_small_or_imprecise_dtypes=True))
-    op("g", ["onesa"], ["dgb"], lambda e: e.affine_select(T.dgb[:], T.ones[:, 0:64], [[-1, 64]], OP.is_equal, 0.0, -64, 1))
-    for i, src, add in ((0, "phi", 0.0), (32, "phi", 128.0), (64, "plo", 0.0)):
-        op("a", [src, "xx0z"], ["xx0"], lambda e: e.activation(T.xx0[:, i:i + 16:5], T[src][:], AF.Copy, bias=add))
+    op("floor", "v", [], ["floor"], V.memset, floor, FLOOR)
+    dma("ut", "s", [], ["ut"], "ld0", T.ut[:, 0:4], T.u[:, 0:4])
+    dma("gr0", "s", [], ["gr0"], "ld1", T.grt[:, 0:512], T.gr[:, 0:512])
+    dma("gr1", "a", ["floor"], ["gr1"], "ld2", T.grt[:, 512:1024], T.gr[:, 512:1024])
+    dma("wt", "s", ["gr1"], ["wt"], "ld3", T.wt[:], T.w[:])
+
+    op("pi", "g", [], ["pi"], g.iota, T.pi[:, 0:1], [[0, 1]], 0, 1)
+    op("ldz", "v", [], ["ldz"], V.memset, T.ldz[:], BELOW)
+    op("m4", "v", [], ["m4"], V.memset, T.m4[:], MAGIC)
+    op("onesa", "v", [], ["onesa"], V.memset, T.ones[:, 96:224], 1.0)
+    op("onesb", "v", [], ["onesb"], V.memset, T.ones[:, 224:616], 1.0)
+    op("pf", "v", ["pi"], ["pf"], V.tensor_copy, pf, T.pi[:, 0:1])
+    op("phi", "v", ["m4", "pf"], ["phi"], V.tensor_scalar, T.phi[:], T.m4[:], pf, MAGIC, OP.add, OP.subtract)
+    op("ph128", "v", ["m4", "pf"], ["ph128"], V.tensor_scalar, T.ph128[:], T.m4[:], pf, MAGIC - 128.0, OP.add, OP.subtract)
+    op("plo", "v", ["phi", "pf"], ["plo"], V.tensor_scalar, T.plo[:], T.phi[:], pf, -1.0, OP.subtract, OP.mult)
+    op("ld0", "g", ["ldz"], ["ld0"], g.affine_select, T.ld0[:], T.ldz[:], [[-1, 128]], OP.is_gt, 1.0, 0, 1)
+    op("hp", "g", [], ["hp"], g.iota, T.hp[:], [[0, 8], [1, 16], [16, 4]], 0, 0, **loose)
+    op("pat0", "v", [], ["pat0"], V.memset, T.pat[:], 0.0)
+    for k, at, val in ((1, slice(0, 16, 5), 1.0), (2, slice(16, 22, 5), 1.0), (3, slice(18, 24, 5), 256.0)):
+        op("pat%d" % k, "v", ["pat0"], ["pat%d" % k], V.memset, T.pat[:, at], val)
+    for i, src in ((0, "phi"), (32, "ph128"), (64, "plo")):
+        op("xa%d" % i, "a", [src, "pat1", "pat2", "pat3"], ["xa%d" % i], A.activation, T.ones[:, i:i + 32], T.pat[:], AF.Copy, scale=T[src][:, 0:1])
+    op("qx0", "v", ["xa0", "xa32", "xa64", "onesa", "onesb"], ["qx0"], V.quantize_mx, T.qx0[:], T.sx0[:], T.ones[:, 0:576])
     for t in range(4):
-        op("v", ["onesa", "ut"], ["ur"], lambda e: e.tensor_scalar(T.ur[:, t:512:4], T.ones[:, 0:128], T.ut[:, t:t + 1], None, OP.mult))
+        op("ur%d" % t, "v", ["onesa", "ut"], ["ur%d" % t], V.tensor_scalar, T.ur[:, t:512:4], T.ones[:, 96:224], T.ut[:, t:t + 1], None, OP.mult)
     H = [slice(0, 128), slice(128, 256)]
-    op("v", ["gr0"], ["qg0"], lambda e: e.quantize_mx(T.qg[:, H[0]], T.sg[:, H[0]], T.grt[:, 0:512]))
-    op("v", ["ur"], ["qu"], lambda e: e.quantize_mx(T.qu[:], T.su[:], T.ur[:]))
-    op("v", ["gr1"], ["qg1"], lambda e: e.quantize_mx(T.qg[:, H[1]], T.sg[:, H[1]], T.grt[:, 512:1024]))
-    op("v", ["xx0"], ["qx0"], lambda e: e.quantize_mx(T.qx0[:], T.sx0[:], T.xx0[:]))
-
-    def unpacker(t):
-        op("v", ["zd"], ["qe"], lambda e: e.quantize_mx(T.qe[:, 128 * t:128 * t + 128], T.se[:, 128 * t:128 * t + 128], T.zd[:, 3 - t:515 - t]))
-
-    def zeros(b):
-        z, s = T["z%d" % b], T["sz%d" % b]
-        op("v", ["zer"], ["z%dm" % b], lambda e: e.quantize_mx(z[:, 256:384], s[:, 256:384], T.zer[:]))
-        op("v", ["zer"], ["z%dz" % b], lambda e: e.quantize_mx(z[:, 0:128], s[:, 0:128], T.zer[:]))
-
+    op("qu", "v", ["ur0", "ur1", "ur2", "ur3"], ["qu"], V.quantize_mx, T.qu[:], T.su[:], T.ur[:])
+    op("qg0", "v", ["gr0"], ["qg0"], V.quantize_mx, T.qg[:, H[0]], T.sg[:, H[0]], T.grt[:, 0:512])
+    op("qg1", "v", ["gr1"], ["qg1"], V.quantize_mx, T.qg[:, H[1]], T.sg[:, H[1]], T.grt[:, 512:1024])
     for h, P in ((0, "PC"), (1, "PS")):
-        op("t", ["qu", "qg%d" % h], [P], lambda e: e.matmul_mx(T[P][:, 0:128], T.qg[:, H[h]], T.sg[:, H[h]], T.qu[:], T.su[:], True, True))
-        op("t", ["qu", "qg%d" % h], ["PE%d" % h], lambda e: e.matmul_mx(T.PE[:, 512 * h:512 * h + 128], T.qu[:], T.su[:], T.qg[:, H[h]], T.sg[:, H[h]], True, True))
-        op("a", [P, "floor"], ["sc0%d" % h], lambda e: e.activation(T.sc0[:, h:h + 1], T[P][:, 0:1], AF.Abs, bias=floor))
-        op("a", ["PE%d" % h, "floor"], ["sr0%d" % h], lambda e: e.activation(T.sr0[:, H[h]], T.PE[:, 512 * h:512 * h + 128], AF.Abs, bias=floor))
-
-    def across(h):
-        op("v", ["sr0%d" % (1 - h), "sc0%d" % h], ["c%da" % h], lambda e: e.tensor_scalar(
-            T["c%d" % h][:, H[1 - h]], T.sr0[:, H[1 - h]], T.sc0[:, h:h + 1], None, OP.is_ge if h else OP.is_gt))
-
-    def passed(h):
-        op("v", ["ld0", "sc0%d" % h], ["d%d" % h], lambda e: e.tensor_scalar(T["d%d" % h][:], T.ld0[:], T.sc0[:, h:h + 1], None, OP.mult))
-
-    def within(h):
-        op("v", ["sr0%d" % h, "d%d" % h], ["c%db" % h], lambda e: e.tensor_tensor(T["c%d" % h][:, H[h]], T.sr0[:, H[h]], T["d%d" % h][:], OP.is_gt))
-
-    def total(h, k, i):
-        part = H[1 - h] if k == "a" else H[h]
-        op("a", ["c%d%s" % (h, k)], ["rk%d%s" % (h, k), "cx%d%s" % (h, k)], lambda e: e.activation(
-            T["c%d" % (h + 2)][:, part], T["c%d" % h][:, part], AF.Copy, accum_out=T.rk0[:, i:i + 1]))
-
-    def onehot(h):
-        op("v", ["hp", "rk%da" % h, "rk%db" % h], ["ht0%d" % h], lambda e: e.tensor_scalar(
-            T.ht0[:, 512 * h:512 * h + 512], T.hp[:], T.rk0[:, 2 * h:2 * h + 1], T.rk0[:, 2 * h + 1:2 * h + 2], OP.subtract, OP.is_equal))
-
-    op("v", ["pi"], ["pi15"], lambda e: e.tensor_scalar(T.pi[:, 1:2], T.pi[:, 0:1], 15, None, OP.bitwise_and))
-    unpacker(0)
-    passed(0)
-    op("v", ["pi15"], ["pm"], lambda e: e.tensor_copy(pm, T.pi[:, 1:2]))
-    op("v", ["kr"], ["rst"], lambda e: e.tensor_scalar(T.rst[:], T.kr[:], 0.5, None, OP.is_gt))
-    within(0)
-    passed(1)
-    across(0)
-    across(1)
-    within(1)
-    total(0, "b", 0)
-    total(0, "a", 1)
-    total(1, "a", 2)
-    total(1, "b", 3)
-    unpacker(1)
-    onehot(0)
-    op("v", ["kr", "pm"], ["mask"], lambda e: e.tensor_scalar(T.mask[:], T.kr[:], pm, None, OP.is_equal))
-    onehot(1)
+        mm("col%d" % h, ["qu", "qg%d" % h], P, T[P][:, 0:128], "qg", 128 * h, "qu", 0)
+        mm("row%d" % h, ["qu", "qg%d" % h], "PE%d" % h, T.PE[:, 512 * h:512 * h + 128], "qu", 0, "qg", 128 * h)
+        op("sc%d" % h, "a", [P, "floor"], ["sc%d" % h], A.activation, T.sc0[:, h:h + 1], T[P][:, 0:1], AF.Abs, bias=floor)
+        op("sr%d" % h, "a", ["PE%d" % h, "floor"], ["sr%d" % h], A.activation, T.sr0[:, H[h]], T.PE[:, 512 * h:512 * h + 128], AF.Abs, bias=floor)
+        op("d%d" % h, "v", ["ld0", "sc%d" % h], ["d%d" % h], V.tensor_scalar, T["d%d" % h][:], T.ld0[:], T.sc0[:, h:h + 1], None, OP.mult)
     for h in range(2):
-        op("v", ["ht0%d" % h], ["qh0%d" % h], lambda e: e.quantize_mx(T.qh0[:, H[h]], T.sh0[:, H[h]], T.ht0[:, 512 * h:512 * h + 512]))
+        op("wi%d" % h, "v", ["sr%d" % h, "d%d" % h], ["wi%d" % h], V.tensor_tensor, T["c%d" % h][:, H[h]], T.sr0[:, H[h]], T["d%d" % h][:], OP.is_gt)
+        op("ac%d" % h, "v", ["sr%d" % (1 - h), "sc%d" % h], ["ac%d" % h], V.tensor_scalar,
+           T["c%d" % h][:, H[1 - h]], T.sr0[:, H[1 - h]], T.sc0[:, h:h + 1], None, OP.is_ge if h else OP.is_gt)
+        for k, part, i in (("ac", H[1 - h], 2 * h), ("wi", H[h], 2 * h + 1)):
+            name = "t%s%d" % (k, h)
+            if name == "twi1":
+                op(name, "v", [k + str(h)], [name], V.tensor_reduce, T.rk0[:, i:i + 1], T["c%d" % h][:, part], X, OP.add)
+            else:
+                op(name, "a", [k + str(h)], [name], A.activation, T["c%d" % (h + 2)][:, part], T["c%d" % h][:, part], AF.Copy, accum_out=T.rk0[:, i:i + 1])
+        op("ht%d" % h, "v", ["hp", "tac%d" % h, "twi%d" % h], ["ht%d" % h], V.tensor_scalar,
+           T.ht0[:, 512 * h:512 * h + 512], T.hp[:], T.rk0[:, 2 * h:2 * h + 1], T.rk0[:, 2 * h + 1:2 * h + 2], OP.subtract, OP.is_equal)
+        op("qh%d" % h, "v", ["ht%d" % h], ["qh%d" % h], V.quantize_mx, T.qh0[:, H[h]], T.sh0[:, H[h]], T.ht0[:, 512 * h:512 * h + 512])
         for c in (8 * h, 16):
-            op("t", ["qh0%d" % h, "qx0"], ["PL"], lambda e: e.matmul_mx(
-                T.PL[:, 0:128], T.qh0[:, H[h]], T.sh0[:, H[h]], T.qx0[:, c:c + 128], T.sx0[:, c:c + 128], h == 0 and c == 0, h == 1 and c == 16))
-    zeros(0)
-    unpacker(2)
-    unpacker(3)
-    op("v", [], ["daz"], lambda e: e.memset(T.m_da[:, 64:320:80], 0.0))
-    op("v", ["PL"], ["lst0"], lambda e: e.tensor_copy(T.lst0[:, 0:4], T.PL[:, 0:4]))
-    op("v", [], ["neg1"], lambda e: e.memset(T.neg1[:], -1.0))
-    op("v", ["hp", "pm"], ["jc"], lambda e: e.tensor_scalar(T.jc[:], T.hp[:, 0:4], pm, None, OP.add))
+            mm("ls%d_%d" % (h, c), ["qh%d" % h, "qx0"], "PL", T.PL[:, 0:128], "qh0", 128 * h, "qx0", c, 128, h == 0 and c == 0, h == 1 and c == 16)
+    op("lst0", "v", ["PL"], ["lst0"], V.tensor_copy, T.lst0[:, 0:6], T.PL[:, 0:6])
+    op("zer", "v", [], ["zer"], V.memset, T.zer[:], 0.0)
+    for b in (1, 2):
+        op("zz%d" % b, "v", ["zer"], ["z%dz" % b], V.quantize_mx, T["z%d" % b][:, 0:128], T["sz%d" % b][:, 0:128], T.zer[:])
 
     def pick(b, into, at):
         src, ssrc, w, frm = (("qg", "sg", slice(0, 256), ["qg0", "qg1"]) if b == 0 else
-                             ("z%d" % (b - 1), "sz%d" % (b - 1), slice(128, 320), ["z%d%s" % (b - 1, k) for k in "psom"]))
+                             ("z%d" % (b - 1), "sz%d" % (b - 1), slice(64, 256), ["z%d%s" % (b - 1, k) for k in "psom"]))
         lst = "lst%d" % b
-        op("v", frm + [lst], [into + "o"], lambda e: e.tensor_copy(
-            T[into][:, at].bitcast(dt.uint32), T[src][:, w].bitcast(dt.uint32).indirect(T[lst][:, 0:4])))
-        op("a", frm + [lst], [into + "s"], lambda e: e.activation(T["s" + into][:, at], T[ssrc][:, w].indirect(T[lst][:, 0:4]), AF.Copy))
+        frm = frm + [lst] + ([into + "z"] if b in (1, 2) else [])
+        op(into + "o", "v", frm, [into + "o"], V.tensor_copy,
+           T[into][:, at].bitcast(dt.uint32), T[src][:, w].bitcast(dt.uint32).indirect(T[lst][:, 0:4]))
+        op(into + "s", "a", frm, [into + "s"], A.activation, T["s" + into][:, at], T[ssrc][:, w].indirect(T[lst][:, 0:4]), AF.Copy)
 
     ha, hb = helpers(rank)
     away = T.cores[rank ^ 2]
-    ready("g", ["lst0"])
-    send(T.hl[:], T.lst0[:, 0:4], hb, "hl", away)
+    remote("sl0", ["lst0"], send, T.hl[:], T.lst0[:, 4:6], hb, "hl", away)
     pick(0, "z0", OWN)
-    ready("g", ["z0o"])
-    send(bits(T.hc[:]), bits(T.z0[:, OWN]), ha, "hc", away)
-    ready("g", ["z0s"])
-    send(T.hs[:], T.sz0[:, OWN], hb, "hs", away)
+    remote("sc_0", ["z0o"], send, bits(T.hc[:]), bits(T.z0[:, OWN]), ha, "hc", away)
+    remote("ss0", ["z0s"], send, T.hs[:], T.sz0[:, OWN], hb, "hs", away)
 
-    def big(b):
-        op("g", ["iot"], ["t4%d" % b], lambda e: e.affine_select(T["t4%d" % b][:], T.iot[:], [[0, 256]], OP.is_gt, BIG, -1, 0))
-
-    def own_tables(b, aw, awt):
-        z, s, zt = T["z%d" % b], T["sz%d" % b], ["z%d%s" % (b, k) for k in "osm"]
-        op("v", ["iot", awt, "t1%d" % b], ["t1%d" % b], lambda e: e.tensor_copy(T["t1%d" % b][:].indirect(aw), T.iot[:, 0:64]))
-        op("a", ["iot", awt], ["nra"], lambda e: e.activation(T.m_nr[:, 0:64], T.iot[:].indirect(aw), AF.Copy))
-        op("g", ["nra"], ["dxa"], lambda e: e.affine_select(T.m_dx[:, 0:64], T.m_nr[:, 0:64], [[-1, 64]], OP.is_equal, 0.0, 0, 1))
-        if b == 0:
-            big(0)
-        for t in range(4):
-            op("t", ["qe"] + zt, ["PE%d" % t], lambda e: e.matmul_mx(
-                T.PE[:, 512 * t:512 * t + 128], T.qe[:, 128 * t:128 * t + 128], T.se[:, 128 * t:128 * t + 128], z[:, 192:320], s[:, 192:320], True, True))
-            op("a", ["PE%d" % t, "daz"], ["da%d" % t], lambda e: e.activation(T.m_da[:, 80 * t:80 * t + 64], T.PE[:, 512 * t:512 * t + 64], AF.Copy))
-        op("t", ["qu"] + zt, ["PR"], lambda e: e.matmul_mx(T.PR[:, 0:128], T.qu[:], T.su[:], z[:, 192:320], s[:, 192:320], True, True))
-
-    own_tables(0, T.lst0[:, 0:4], "lst0")
-    op("v", ["pf"], ["nisa"], lambda e: e.tensor_scalar(nisa, pf, 63.5, -1.0, OP.is_lt, OP.mult))
-    op("v", ["pf"], ["okb"], lambda e: e.tensor_scalar(okb, pf, 63.5, 1.0, OP.is_lt, OP.add))
-    op("v", ["phi"], ["ph64"], lambda e: e.tensor_scalar(T.ph64[:], T.phi[:], 64.0, None, OP.add))
-    op("v", [], ["mtz"], lambda e: e.memset(T.m_mt[:, 256:512], 0.0))
-    op("v", [], ["xxz"], lambda e: e.memset(T.xx[:], 0.0))
-    zeros(1)
-    op("v", ["plo", "xxz"], ["xxl"], lambda e: e.tensor_copy(T.xx[:, 48:64:5], T.plo[:]))
+    op("zd", "g", ["onesa", "onesb"], ["zd"], g.affine_select, T.zd[:, 0:516], T.ones[:, 96:612], [[-1, 516]], OP.is_equal, 0.0, 3, 4)
+    op("iot", "g", [], ["iot"], g.iota, T.iot[:], [[1, 256]], 0, 0, **loose)
+    op("kr", "g", [], ["kr"], g.iota, T.kr[:], [[0, 4], [1, 16]], 0, 0, **loose)
+    op("dgb", "g", ["onesa"], ["dgb"], g.affine_select, T.dgb[:], T.ones[:, 96:160], [[-1, 64]], OP.is_equal, 0.0, -64, 1)
+    for b in range(3):
+        op("tz%d" % b, "g", [], ["t1%d" % b], g.iota, T["t1%d" % b][:], [[1, 256]], 128, 0, **loose)
+    op("ptz", "g", [], ["ptz"], g.iota, T.pt[:], [[0, 512]], 0, 0, **loose)
+    op("rwz", "g", [], ["rwz"], g.iota, T.m_rw[:, 64:384], [[0, 320]], 0, 0, **loose)
+    for t in range(4):
+        op("qe%d" % t, "v", ["zd"], ["qe%d" % t], V.quantize_mx, T.qe[:, 128 * t:128 * t + 128], T.se[:, 128 * t:128 * t + 128], T.zd[:, 3 - t:515 - t])
+    op("daz", "v", [], ["daz"], V.memset, T.m_da[:, 256:576], 0.0)
+    op("pi15", "v", ["pi"], ["pi15"], V.tensor_scalar, T.pi[:, 1:2], T.pi[:, 0:1], 15, None, OP.bitwise_and)
+    op("pm", "v", ["pi15"], ["pm"], V.tensor_copy, pm, T.pi[:, 1:2])
+    op("rst", "v", ["kr"], ["rst"], V.tensor_scalar, T.rst[:], T.kr[:], 0.5, None, OP.is_gt)
+    op("mask", "v", ["kr", "pm"], ["mask"], V.tensor_scalar, T.mask[:], T.kr[:], pm, None, OP.is_equal)
+    op("jc", "v", ["hp", "pm"], ["jc"], V.tensor_scalar, T.jc[:], T.hp[:, 0:4], pm, None, OP.add)
+    op("vvc", "v", ["pf"], ["vvc"], V.tensor_scalar, T.m_vv[:, 64:65], pf, 63.5, BIG, OP.is_lt, OP.mult)
+    op("n4", "v", [], ["n4"], V.memset, T.n4[:], 64.0)
+    op("cut", "v", [], ["cut"], V.memset, T.m_cc[:, 64:65], -63.5)
+    op("off", "v", ["pf"], ["off"], V.tensor_scalar, off, pf, 63.5, -16.0, OP.is_gt, OP.mult)
+    op("huge", "v", [], ["huge"], V.memset, huge, HUGE)
+    op("mtz", "v", [], ["mtz"], V.memset, T.m_mt[:, 256:512], 0.0)
+    op("xxz", "v", [], ["xxz"], V.memset, T.xx[:], 0.0)
+    op("xxl", "v", ["plo", "xxz"], ["xxl"], V.tensor_copy, T.xx[:, 48:64:5], T.plo[:])
+    op("qn", "v", ["onesa", "onesb"], ["qn"], V.quantize_mx, T.qn[:], T.sn[:], T.ones[:, 96:608])
+    op("qw", "v", ["wt"], ["qw"], V.quantize_mx, T.qw[:], T.sw[:], T.wt[:])
 
     for b in range(3):
-        nx = b + 1
-        z, sz = T["z%d" % b], T["sz%d" % b]
-        own, mrg, prt = ["z%do" % b, "z%ds" % b], "z%dm" % b, "z%dp" % b
-        t1, t4 = "t1%d" % b, "t4%d" % b
+        nx, B = b + 1, ".%d" % b
+        zn = "z%d" % b
+        z, sz = T[zn], T["s" + zn]
+        own, mrg, prt = [zn + "o", zn + "s"], zn + "m", zn + "p"
+        t1 = "t1%d" % b
         aw, awt = (T.lst0[:, 0:4], "lst0") if b == 0 else (T["lst%d" % b][:, 4:8], "lst%d" % b)
+
+        op("t1" + B, "v", ["iot", awt, t1], [t1], V.tensor_copy, T[t1][:].indirect(aw), T.iot[:, 0:64])
+        op("nra" + B, "a", ["iot", awt], ["nra"], A.activation, T.m_nr[:, 0:64], T.iot[:].indirect(aw), AF.Copy)
+        op("dxa" + B, "g", ["nra"], ["dxa"], g.affine_select, T.m_dx[:, 0:64], T.m_nr[:, 0:64], [[-1, 64]], OP.is_equal, 0.0, 0, 1)
+        op("nca" + B, "a", ["dxa", "off"], ["nca", "dya"], A.activation, T.m_dy[:, 128:192], T.m_dx[:, 0:64], AF.Identity, bias=off, accum_out=nca)
+        for t in range(4):
+            if b == 0:
+                mm("uo%d" % t + B, ["qe%d" % t, "qg0", "qg1"], "PE%d" % t, T.PE[:, 512 * t:512 * t + 256], "qe", 128 * t, "qg", 0, 256)
+                op("da%d" % t + B, "a", ["PE%d" % t], ["dn%d" % t], A.activation, T.m_dn[:, 256 * t:256 * t + 256], T.PE[:, 512 * t:512 * t + 256], AF.Copy)
+                continue
+            mm("uo%d" % t + B, ["qe%d" % t, zn + "z"] + own, "PE%d" % t, T.PE[:, 512 * t:512 * t + 128], "qe", 128 * t, zn, 0)
+            plane, bank = T.m_da[:, 64 * t:64 * t + 64], T.PE[:, 512 * t + 64:512 * t + 128]
+            if t < 2:
+                op("da%d" % t + B, "a", ["PE%d" % t], ["da%d" % t], A.activation, plane, bank, AF.Copy)
+            else:
+                op("da%d" % t + B, "v", ["PE%d" % t], ["da%d" % t], V.tensor_copy, plane, bank)
+        if b:
+            mm("ro" + B, ["qu", zn + "z"] + own, "PR", T.PR[:, 0:128], "qu", 0, zn, 0)
+            op("rw" + B, "a", ["PR", "floor"], ["rw"], A.activation, T.m_rw[:, 0:64], T.PR[:, 64:128], AF.Abs, bias=floor)
+
         src = helpers(rank ^ 1)[0] if b == 0 else T.cores[rank ^ (1 << b)]
         n = len(topo.engines(src, core))
         arrives("bl%d" % b, "al%d" % b, n)
         arrives(prt, "ac%d" % b, 2 * n)
 
-        if b == 2:
-            op("v", ["bl2"], ["bi"], lambda e: e.tensor_copy(T.bi[:, 0:2], T.bl2[:]))
-            op("v", ["bi"], ["bj0"], lambda e: e.tensor_scalar(T.bj[:, 0:2], T.bi[:, 0:2], 255, None, OP.bitwise_and))
-            op("v", ["bi"], ["bj1"], lambda e: e.tensor_scalar(T.bj[:, 2:4], T.bi[:, 0:2], 8, None, OP.logical_shift_right))
-            op("v", ["bj0", "bj1"], ["bu"], lambda e: e.tensor_copy(T.bu[:], T.bj[:, 0:4]))
-        bwt = "bl%d" % b if b < 2 else "bu"
+        if b == 0:
+            op("bi", "v", ["bl0"], ["bi"], V.tensor_copy, T.bi[:, 0:2], T.bl0[:])
+            op("bj0", "v", ["bi"], ["bj0"], V.tensor_scalar, T.bj[:, 0:2], T.bi[:, 0:2], 255, None, OP.bitwise_and)
+            op("bj1", "v", ["bi"], ["bj1"], V.tensor_scalar, T.bj[:, 2:4], T.bi[:, 0:2], 8, None, OP.logical_shift_right)
+            op("bu", "v", ["bj0", "bj1"], ["bu"], V.tensor_copy, T.bu[:], T.bj[:, 0:4])
+        bwt = "bl%d" % b if b else "bu"
         bw = T[bwt][:]
-        op("v", [t1, bwt, "mask"], ["g4"], lambda e: e.tensor_tensor(T.m_g4[:], T[t1][:].indirect(bw), T.mask[:], OP.mult))
-        op("v", ["iot", bwt, "dgb"], ["dxb"], lambda e: e.tensor_tensor(T.m_dx[:, 64:128], T.iot[:].indirect(bw), T.dgb[:], OP.mult))
-        op("v", ["g4", "rst"], ["g5"], lambda e: e.tensor_tensor_scan(T.m_g5[:], T.rst[:], T.m_g4[:], 0.0, OP.mult, OP.add))
-        op("v", [t1, bwt, "dgb"], ["vv"], lambda e: e.tensor_tensor(T.m_vv[:], T[t1][:].indirect(bw), T.dgb[:], OP.mult))
-        op("v", ["g5"], ["toff"], lambda e: e.tensor_copy(T.m_toff[:], T.m_g5[:, 15:64:16]))
-        op("v", ["g5"], ["fa"], lambda e: e.tensor_scalar(T.m_fa[:], T.m_g5[:, 15:64:16], 63.5, 64.0, OP.is_lt, OP.mult))
-        op("v", ["vv"], ["v"], lambda e: e.tensor_reduce(v, T.m_vv[:], X, OP.add))
-        op("a", ["iot", bwt], ["nrb"], lambda e: e.activation(T.m_nr[:, 64:128], T.iot[:].indirect(bw), AF.Copy))
-        op("a", ["dxa", "dxb"], ["nc", "dy"], lambda e: e.activation(T.m_dy[:], T.m_dx[:], AF.Copy, accum_out=nc))
-        if b < 2:
-            op("g", [], ["t1%d" % nx], lambda e: e.iota(T["t1%d" % nx][:], [[0, 256]], 64, 0, allow_small_or_imprecise_dtypes=True))
-            big(nx)
-        if b == 0:
-            op("g", [], ["ptz"], lambda e: e.iota(T.pt[:], [[0, 512]], 0, 0, allow_small_or_imprecise_dtypes=True))
+        op("g4" + B, "v", [t1, bwt, "mask"], ["g4"], V.tensor_tensor, T.m_g4[:], T[t1][:].indirect(bw), T.mask[:], OP.mult)
+        op("g5" + B, "v", ["g4", "rst"], ["g5"], V.tensor_tensor_scan, T.m_g5[:], T.rst[:], T.m_g4[:], 0.0, OP.mult, OP.add)
+        if b:
+            op("toff" + B, "v", ["g5"], ["toff"], V.tensor_copy, T.m_toff[:], T.m_g5[:, 15:64:16])
+        op("fa" + B, "v", ["g5"], ["fa"], V.tensor_scalar, T.m_fa[:], T.m_g5[:, 15:64:16], 63.5, 64.0, OP.is_lt, OP.mult)
+        op("vv" + B, "v", [t1, bwt, "dgb"], ["vv"], V.tensor_tensor, T.m_vv[:, 0:64], T[t1][:].indirect(bw), T.dgb[:], OP.mult)
+        op("v" + B, "v", ["vv", "vvc"], ["v"], V.tensor_reduce, v, T.m_vv[:, 0:65], X, OP.add)
+        op("nrb" + B, "a", ["iot", bwt], ["nrb"], A.activation, T.m_nr[:, 64:128], T.iot[:].indirect(bw), AF.Copy)
+        op("dxb" + B, "v", ["iot", bwt, "dgb"], ["dxb"], V.tensor_tensor, T.m_dx[:, 64:128], T.iot[:].indirect(bw), T.dgb[:], OP.mult)
+        op("nc" + B, "a", ["dxa", "dxb"], ["nc", "dy"], A.activation, T.m_dy[:, 0:128], T.m_dx[:], AF.Copy, accum_out=nc)
         for t in range(4):
-            pa, da = T.m_pa[:, 64 * t:64 * t + 64], T.m_da[:, 80 * t:80 * t + 65].indirect(T.m_toff[:])
-            if t < 2:
-                op("v", ["da%d" % t, "toff"], ["pa%d" % t], lambda e: e.tensor_copy(pa, da))
+            pa = T.m_pa[:, 64 * t:64 * t + 64]
+            if b == 0:
+                da, frm = T.m_dn[:, 256 * t:256 * t + 256].indirect(bw), ["dn%d" % t, bwt]
             else:
-                op("a", ["da%d" % t, "toff"], ["pa%d" % t], lambda e: e.activation(pa, da, AF.Copy))
-        op("v", ["v"], ["hc"], lambda e: e.tensor_scalar(hc, v, 63.5, None, OP.is_gt))
-        op("v", ["v"], ["mc"], lambda e: e.tensor_scalar(mc, v, 63.5, None, OP.is_lt))
-        op("a", ["PR", "floor"], ["rw"], lambda e: e.activation(T.m_rw[:], T.PR[:, 0:64], AF.Abs, bias=floor))
-        op("a", ["nra", "nrb", "nc"], ["eq"], lambda e: e.activation(T.m_eq[:], T.m_nr[:], AF.Abs, bias=nc, scale=-1.0))
-        op("a", ["eq"], ["cnt", "eq2"], lambda e: e.activation(T.m_eq2[:], T.m_eq[:], AF.Relu, bias=1.0, scale=-1.0, accum_out=cnt))
+                da, frm = T.m_da[:, 64 * t:64 * t + 384].indirect(T.m_toff[:]), ["da%d" % k for k in range(t, 4)] + ["daz", "toff"]
+            if t < (2 if b else 1):
+                op("pa%d" % t + B, "v", frm, ["pa%d" % t], V.tensor_copy, pa, da)
+            else:
+                op("pa%d" % t + B, "a", frm, ["pa%d" % t], A.activation, pa, da, AF.Copy)
+        op("fb" + B, "v", ["fa", "jc"], ["fb"], V.tensor_tensor, T.m_fb[:], T.m_fa[:], T.jc[:], OP.add)
+        op("fl" + B, "v", ["fb"], ["fl"], V.tensor_copy, T.m_fl[:], T.m_fb[:])
+        op("mc" + B, "v", ["v"], ["mc"], V.tensor_scalar, mc, v, 63.5, None, OP.is_lt)
+        op("hc" + B, "v", ["v"], ["hc"], V.tensor_scalar, hc, v, 63.5, None, OP.is_gt)
+        op("xxh" + B, "v", ["phi", "n4", "mc", "xxz"], ["xxh"], V.tensor_scalar, T.xx[:, 0:16:5], T.n4[:], mc, T.phi[:, 0:1], OP.mult, OP.add)
+        if b < 2:
+            op("xxn" + B, "v", ["m4", "nc", "xxz"], ["xxn"], V.tensor_scalar, T.xx[:, 16:32:5], T.m4[:], nc, MAGIC, OP.add, OP.subtract)
+            op("xxm" + B, "v", ["xxn", "nc"], ["xxm"], V.tensor_scalar, T.xx[:, 64:80:5], T.xx[:, 16:32:5], nc, -1.0, OP.subtract, OP.mult)
+        op("qx" + B, "v", ["xxl", "xxh"] + (["xxn", "xxm"] if b < 2 else []), ["qx"], V.quantize_mx, T.qx[:], T.sx[:], T.xx[:])
+        op("eq" + B, "a", ["iot", bwt, "nca"], ["eq"], A.activation, T.m_eq[:], T.iot[:].indirect(bw), AF.Abs, bias=nca, scale=-1.0)
+        op("eq2" + B, "a", ["eq", "huge"], ["hit", "eq2"], A.activation, T.m_eq2[:], T.m_eq[:], AF.Relu, bias=huge, scale=-HUGE, accum_out=hit)
+        if b == 0:
+            op("strike" + B, "v", ["sr0", "sr1", "zer", bwt], ["sr0", "sr1", "rw"], V.tensor_copy, T.sr0[:].indirect(bw), T.zer[:, 0:64])
+        else:
+            op("strike" + B, "v", ["rw", "rwz", "zer", "toff"], ["rw"], V.tensor_copy, T.m_rw[:].indirect(T.m_toff[:]), T.zer[:, 0:64])
+        op("ga" + B, "v", ["nra", "nc"], ["ga"], V.tensor_scalar, T.m_f[:, 0:64], T.m_nr[:, 0:64], nc, BELOW, OP.is_lt, OP.max)
+        op("wa" + B, "v", ["rw", "ga", awt], ["wa"], V.tensor_tensor, T.m_m[:, 0:64], T.m_rw[:, 0:64] if b else T.sr0[:].indirect(aw),
+           T.m_f[:, 0:64], OP.mult)
+        op("f" + B, "v", ["nrb", "nc"], ["f"], V.tensor_scalar, T.m_f[:, 64:128], T.m_nr[:, 64:128], nc, BELOW, OP.is_ge, OP.max)
 
         for t in range(4):
-            op("t", ["qe", prt] + own, ["PE%d" % t], lambda e: e.matmul_mx(
-                T.PE[:, 512 * t:512 * t + 128], T.qe[:, 128 * t:128 * t + 128], T.se[:, 128 * t:128 * t + 128], z[:, 128:256], sz[:, 128:256], True, True))
-        op("t", ["qu", "z%dz" % b, prt], ["PL"], lambda e: e.matmul_mx(T.PL[:, 0:128], z[:, 64:192], sz[:, 64:192], T.qu[:], T.su[:], True, True))
-        op("t", ["qu", prt] + own, ["PR"], lambda e: e.matmul_mx(T.PR[:, 0:128], T.qu[:], T.su[:], z[:, 128:256], sz[:, 128:256], True, True))
-        for t in (0, 2, 1, 3):
-            op("v", ["PE%d" % t, "pa%d" % t], ["mt%d" % t], lambda e: e.tensor_tensor(
-                T.m_mt[:, t:256:4], T.PE[:, 512 * t:512 * t + 64], T.m_pa[:, 64 * t:64 * t + 64], OP.add))
-        op("v", ["nra", "nrb", "nc"], ["f"], lambda e: e.tensor_scalar(T.m_f[:], T.m_nr[:], nc, BELOW, OP.is_ge, OP.max))
-        op("v", ["fa", "jc"], ["fb"], lambda e: e.tensor_tensor(T.m_fb[:], T.m_fa[:], T.jc[:], OP.add))
-        op("v", ["mt0", "mt1", "mt2", "mt3", "mtz"], [mrg], lambda e: e.quantize_mx(z[:, 256:384], sz[:, 256:384], T.m_mt[:]))
-        op("t", ["qu", mrg] + own, ["PC"], lambda e: e.matmul_mx(T.PC[:, 0:128], z[:, 192:320], sz[:, 192:320], T.qu[:], T.su[:], True, True))
-        op("t", ["qu", mrg] + own, ["PS"], lambda e: e.matmul_mx(T.PS[:, 0:128], T.qu[:], T.su[:], z[:, 192:320], sz[:, 192:320], True, True))
-        op("v", ["PL", "hc"], ["cc"], lambda e: e.tensor_scalar(cc, T.PL[:, 0:1], hc, FLOOR, OP.mult, OP.add))
+            mm("up%d" % t + B, ["qe%d" % t, prt] + own, "PE%d" % t, T.PE[:, 512 * t:512 * t + 128], "qe", 128 * t, zn, 64)
+            op("mt%d" % t + B, "v", ["PE%d" % t, "pa%d" % t], ["mt%d" % t], V.tensor_tensor,
+               T.m_mt[:, t:256:4], T.PE[:, 512 * t + 64:512 * t + 128], T.m_pa[:, 64 * t:64 * t + 64], OP.add)
+        mm("cp" + B, ["qu", prt] + own, "PL", T.PL[:, 0:128], zn, 64, "qu", 0)
+        mm("rp" + B, ["qu", prt] + own, "PR", T.PR[:, 0:128], "qu", 0, zn, 64)
+        op("wp" + B, "a", ["PR", "floor"], ["wp"], A.activation, T.m_w[:, 0:64], T.PR[:, 64:128], AF.Abs, bias=floor)
+        op("cc" + B, "v", ["PL", "hc"], ["cc"], V.tensor_scalar, cc, T.PL[:, 0:1], hc, FLOOR, OP.mult, OP.add)
+        op("qm" + B, "v", ["mt0", "mt1", "mt2", "mt3", "mtz"], [mrg], V.quantize_mx, z[:, 192:320], sz[:, 192:320], T.m_mt[:])
+
+        mm("cm" + B, ["qu", mrg, prt], "PC", T.PC[:, 0:128], zn, 128, "qu", 0)
+        mm("rm" + B, ["qu", mrg, prt], "PS", T.PS[:, 0:128], "qu", 0, zn, 128)
+        op("sc" + B, "a", ["PC", "mc", "cc"], ["sc"], A.activation, sc, T.PC[:, 0:1], AF.Abs, bias=cc, scale=mc)
+        op("wm" + B, "a", ["PS", "floor"], ["wm"], A.activation, T.m_w[:, 64:128], T.PS[:, 64:128], AF.Abs, bias=floor)
+        op("m1" + B, "v", ["f", "sc", "hit"], ["m1"], V.tensor_scalar, T.m_m[:, 64:128], T.m_f[:, 64:128], sc, hit, OP.mult, OP.subtract)
+        op("cca" + B, "v", ["wa", "sc"], ["cca"], V.tensor_scalar, T.m_cc[:, 0:64], T.m_m[:, 0:64], sc, None, OP.is_ge)
+        op("ccb" + B, "v", ["wp", "wm", "fl", "m1"], ["ccb"], V.tensor_tensor, T.m_cc[:, 72:136], T.m_w[:].indirect(T.m_fl[:]), T.m_m[:, 64:128], OP.is_gt)
         if b < 2:
-            op("v", ["m4", "nc", "xxz"], ["xxn"], lambda e: e.tensor_scalar(T.xx[:, 16:32:5], T.m4[:], nc, MAGIC, OP.add, OP.subtract))
+            op("rka" + B, "v", ["cca"], ["rka"], V.tensor_reduce, rk, T.m_cc[:, 0:64], X, OP.add)
+            op("rkb" + B, "v", ["ccb"], ["rkb"], V.tensor_reduce, rkb, T.m_cc[:, 72:136], X, OP.add)
+            op("ht" + B, "v", ["hp", "rka", "rkb"], ["ht"], V.tensor_scalar, T.m_ht[:], T.hp[:], rk, rkb, OP.subtract, OP.is_equal)
         else:
-            op("v", ["nra", "nrb", "nc"], ["gt"], lambda e: e.tensor_scalar(T.m_gt[:], T.m_nr[:], nc, 1000.0, OP.is_le, OP.mult))
-        op("v", ["v"], ["ph"], lambda e: e.tensor_scalar(ph, v, 63.5, -128.0, OP.is_gt, OP.mult))
-        op("v", [t4, "neg1", bwt], [t4], lambda e: e.tensor_copy(T[t4][:].indirect(bw), T.neg1[:]))
-        op("v", ["ph64", "ph", "xxz"], ["xxh"], lambda e: e.tensor_scalar(T.xx[:, 0:16:5], T.ph64[:], ph, None, OP.add))
-        if b < 2:
-            op("v", ["xxn", "nc"], ["xxm"], lambda e: e.tensor_scalar(T.xx[:, 64:80:5], T.xx[:, 16:32:5], nc, -1.0, OP.subtract, OP.mult))
-        op("v", ["fb"], ["fl"], lambda e: e.tensor_copy(T.m_fl[:], T.m_fb[:]))
-        op("v", [t4, "rw", awt], ["sra"], lambda e: e.tensor_tensor(T.m_sra[:], T[t4][:].indirect(aw), T.m_rw[:], OP.min))
-        op("a", ["cnt", "nisa", "okb"], ["ok"], lambda e: e.activation(okc, cnt, AF.Identity, bias=okb, scale=nisa))
-        op("a", ["PR", "floor"], ["wp"], lambda e: e.activation(T.m_w[:, 0:64], T.PR[:, 0:64], AF.Abs, bias=floor))
-
-        op("a", ["PC", "mc", "cc"], ["sc"], lambda e: e.activation(sc, T.PC[:, 0:1], AF.Abs, bias=cc, scale=mc))
-        op("a", ["PS", "floor"], ["wm"], lambda e: e.activation(T.m_w[:, 64:128], T.PS[:, 64:128], AF.Abs, bias=floor))
-        if b == 1:
-            for i in (0, 48):
-                op("a", ["xxn", "xxm"], ["xxp"], lambda e: e.activation(T.xx[:, i + 32:i + 38:5], T.xx[:, i + 16:i + 22:5], AF.Copy))
-                op("a", ["xxn", "xxm"], ["xxp"], lambda e: e.activation(T.xx[:, i + 34:i + 40:5], T.xx[:, i + 16:i + 22:5], AF.Copy, scale=256.0))
-        for k, i in (("m0", 0), ("m1", 64)):
-            op("v", ["f", "sc", "ok"], [k], lambda e: e.tensor_scalar(T.m_m[:, i:i + 64], T.m_f[:, i:i + 64], sc, okc, OP.mult, OP.mult))
-        op("v", ["sra", "m0"], ["cca"], lambda e: e.tensor_tensor(T.m_cc[:, 0:64], T.m_sra[:], T.m_m[:, 0:64], OP.is_gt))
-        op("v", ["wp", "wm", "fl", "m1"], ["ccb"], lambda e: e.tensor_tensor(T.m_cc[:, 64:128], T.m_w[:].indirect(T.m_fl[:]), T.m_m[:, 64:128], OP.is_gt))
-
-        def places():
-            op("v", ["xxl", "xxh", "xxn", "xxm"] + (["xxp"] if b == 1 else []), ["qx"], lambda e: e.quantize_mx(T.qx[:], T.sx[:], T.xx[:]))
-
-        if b < 2:
-            op("v", ["cca"], ["rka"], lambda e: e.tensor_reduce(rk, T.m_cc[:, 0:64], X, OP.add))
-            op("v", ["ccb"], ["rkb"], lambda e: e.tensor_reduce(rkb, T.m_cc[:, 64:128], X, OP.add))
-            places()
-            op("v", ["hp", "rka", "rkb"], ["ht"], lambda e: e.tensor_scalar(T.m_ht[:], T.hp[:], rk, rkb, OP.subtract, OP.is_equal))
-        else:
-            op("v", ["cca", "ccb"], ["rka"], lambda e: e.tensor_reduce(rk, T.m_cc[:], X, OP.add))
-            op("t", ["qw", mrg, prt] + own, ["PE0"], lambda e: e.matmul_mx(T.PE[:, 0:192], T.qw[:], T.sw[:], z[:, 128:320], sz[:, 128:320], True, True))
-            op("a", ["PE0"], ["yt"], lambda e: e.activation(T.ytab[:], T.PE[:, 0:192], AF.Copy))
-            op("a", ["nra", "nrb"], ["nbz0"], lambda e: e.activation(T.nbz[:, 0:64], T.m_nr[:, 64:128], AF.Copy))
-            op("a", ["nra", "nrb"], ["nbz1"], lambda e: e.activation(T.nbz[:, 64:192], T.m_nr[:], AF.Copy))
-            op("v", ["gt", "rka", "ptz"], ["pt"], lambda e: e.tensor_scalar(T.pt[:, 0:512:4], T.m_gt[:], rk, 63.5, OP.add, OP.is_lt))
-            op("v", ["rka"], ["sel"], lambda e: e.tensor_scalar(sel, rk, 63.5, None, OP.is_lt))
-            op("v", ["pt"], ["qp"], lambda e: e.quantize_mx(T.qp[:], T.sp[:], T.pt[:]))
-            places()
-            op("t", ["qp", "qn"], ["PC"], lambda e: e.matmul_mx(T.PC[:, 0:128], T.qp[:], T.sp[:], T.qn[:], T.sn[:], True, True))
-            op("v", ["hp", "PC", "sel"], ["ht"], lambda e: e.tensor_scalar(T.m_ht[:], T.hp[:], T.PC[:, 0:1], sel, OP.is_equal, OP.mult))
-        op("v", ["ht"], ["qh"], lambda e: e.quantize_mx(T.qh[:], T.sh[:], T.m_ht[:]))
+            op("gt", "v", ["nra", "nrb", "nc"], ["gt"], V.tensor_scalar, T.m_gt[:], T.m_nr[:, 0:128], nc, BIG, OP.is_le, OP.mult)
+            op("rka" + B, "v", ["cca", "cut"], ["rka"], V.tensor_reduce, rk, T.m_cc[:, 0:65], X, OP.add)
+            op("rkb" + B, "v", ["ccb"], ["rkb"], V.tensor_reduce, rkb, T.m_cc[:, 72:136], X, OP.add, negate=True)
+            op("pt", "v", ["gt", "rka", "rkb", "ptz"], ["pt"], V.tensor_scalar, T.pt[:, 0:512:4], T.m_gt[:], rk, rkb, OP.add, OP.is_lt)
+            op("sel", "v", ["rka", "rkb"], ["sel"], V.tensor_scalar, sel, rk, rkb, None, OP.is_lt)
+            op("qp", "v", ["pt"], ["qp"], V.quantize_mx, T.qp[:], T.sp[:], T.pt[:])
+            mm("pos", ["qp", "qn"], "PC", T.PC[:, 0:128], "qp", 0, "qn", 0)
+            op("ht" + B, "v", ["hp", "PC", "sel"], ["ht"], V.tensor_scalar, T.m_ht[:], T.hp[:], T.PC[:, 0:1], sel, OP.is_equal, OP.mult)
+            mm("ymm", ["qw", mrg, prt] + own, "PE0", T.PE[:, 0:192], "qw", 0, zn, 64, 192)
+            op("yt", "a", ["PE0"], ["yt"], A.activation, T.ytab[:], T.PE[:, 0:192], AF.Copy)
+            op("nrc", "a", ["nrb"], ["nrc"], A.activation, T.m_nr[:, 128:192], T.m_nr[:, 64:128], AF.Copy)
+        op("qh" + B, "v", ["ht"], ["qh"], V.quantize_mx, T.qh[:], T.sh[:], T.m_ht[:])
         for c in (0, 12):
-            op("t", ["qh", "qx"], ["PL"], lambda e: e.matmul_mx(T.PL[:, 0:128], T.qh[:], T.sh[:], T.qx[:, c:c + 128], T.sx[:, c:c + 128], c == 0, c == 12))
-        if b == 0:
-            zeros(2)
-        if b == 1:
-            op("v", ["onesa", "onesb"], ["qn"], lambda e: e.quantize_mx(T.qn[:], T.sn[:], T.ones[:, 0:512]))
-            op("v", ["wt"], ["qw"], lambda e: e.quantize_mx(T.qw[:], T.sw[:], T.wt[:]))
+            mm("ls%d" % c + B, ["qh", "qx"], "PL", T.PL[:, 0:128], "qh", 0, "qx", c, 128, c == 0, c == 12)
         lst = "lst%d" % nx
-        k = (8, 10, 4)[b]
-        op("v", ["PL"], [lst], lambda e: e.tensor_copy(T[lst][:, 0:k], T.PL[:, 0:k]))
+        k = 8 if b < 2 else 4
+        op(lst, "v", ["PL"], [lst], V.tensor_copy, T[lst][:, 0:k], T.PL[:, 0:k])
         if b < 2:
             to = T.cores[rank ^ (1 << nx)]
-            ready("g", [lst])
-            send(T["bl%d" % nx][:], T[lst][:, 4:8] if b == 0 else T[lst][:, 8:10], to, "al%d" % nx)
             o = "z%d" % nx
+            remote("sl%d" % nx, [lst], send, T["bl%d" % nx][:], T[lst][:, 4:8], to, "al%d" % nx)
             pick(nx, o, OWN)
-            ready("g", [o + "o"])
-            send(bits(T[o][:, PARTNER]), bits(T[o][:, OWN]), to, "ac%d" % nx)
-            ready("g", [o + "s"])
-            send(T["s" + o][:, PARTNER], T["s" + o][:, OWN], to, "ac%d" % nx)
-            own_tables(nx, T[lst][:, 4:8], lst)
+            remote("sc_%d" % nx, [o + "o"], send, bits(T[o][:, PARTNER]), bits(T[o][:, OWN]), to, "ac%d" % nx)
+            remote("ss%d" % nx, [o + "s"], send, T["s" + o][:, PARTNER], T["s" + o][:, OWN], to, "ac%d" % nx)
 
     pick(3, "y3", slice(0, 64))
-    dma("s", ["y3o"], [], "st0", T.oc[:], bits(T.y3[:]))
-    op("v", ["yt", "lst3"], ["ys"], lambda e: e.tensor_copy(T.ys[:], T.ytab[:].indirect(T.lst3[:, 0:4])))
-    op("a", ["nbz0", "nbz1", "lst3"], ["nbs"], lambda e: e.activation(T.nbs[:], T.nbz[:].indirect(T.lst3[:, 0:4]), AF.Copy))
-    dma("a", ["y3s"], [], "st1", T.osc[0:4, :], T.sy3[0:4, :])
-    dma("s", ["ys"], [], "st6", T.y[:], T.ys[:])
-    dma("a", ["y3s"], [], "st2", T.osc[4:8, :], T.sy3[32:36, :])
-    dma("a", ["y3s"], [], "st3", T.osc[8:12, :], T.sy3[64:68, :])
-    dma("s", ["nbs"], [], "st5", T.nb[:], T.nbs[0:1, :])
-    dma("a", ["y3s"], [], "st4", T.osc[12:16, :], T.sy3[96:100, :])
-    finish()
+    dma("oc", "s", ["y3o"], [], "st", T.oc[:], bits(T.y3[:]))
+    op("ys", "v", ["yt", "lst3"], ["ys"], V.tensor_copy, T.ys[:], T.ytab[:].indirect(T.lst3[:, 0:4]))
+    op("nbs", "v", ["nra", "nrb", "nrc", "lst3"], ["nbs"], V.tensor_copy, T.nbs[:], T.m_nr[:].indirect(T.lst3[:, 0:4]))
+    for k in range(4):
+        dma("osc%d" % k, "a", ["y3s"], [], "st", T.osc[4 * k:4 * k + 4, :], T.sy3[32 * k:32 * k + 4, :])
+    dma("y", "s", ["ys"], [], "st", T.y[:], T.ys[:])
+    dma("nb", "s", ["nbs"], [], "st", T.nb[:], T.nbs[0:1, :])
+    left = issue()
     g.wait_ge(T.sem.sent, sent[0])
+    for sem, val in sorted(left, key=lambda x: x[0] == "st"):
+        g.wait_ge(T.sem[sem], val)

from concourse.mybir import dt, AluOpType as OP, AxisListType, ActivationFunctionType as AF

BIG = 1000.0
HUGE = 2.0 ** 90
FLOOR = 2.0 ** -124
BELOW = 1.0 - 2.0 ** -24
MAGIC = 1.5 * 2.0 ** 27

F32, B16, I32, U16, U8, MX = "float32", "bfloat16", "int32", "uint16", "uint8", "float8_e4m3fn_x4"
SCRATCH = {}
for _d, _names in (
        (B16, "ut 16|grt 1024|wt 512|ones 616|pat 32|zer 512|ur 512|zd 520|iot 256|hp 512|kr 64|dgb 64|xx 560"
              "|pt 512|c0 256|c1 256|c2 256|c3 256|ht0 1024|m_nr 192|m_dx 128|m_dy 192"
              "|m_gt 128|m_da 576|m_dn 1024|m_pa 256|m_mt 512|m_ht 512"),
        (F32, "cst 16|mask 64|rst 64|m4 4|n4 4|phi 4|plo 4|ph128 4|jc 4|sr0 256|sc0 8|ld0 128|ldz 128|d0 128|d1 128|rk0 8"
              "|nbs 64|ys 64|ytab 192|t10 256|t11 256|t12 256|m_c 16|m_r 8|m_sc 8|m_v 16|m_eq 64|m_eq2 64|m_g4 64|m_g5 64|m_fa 4|m_fb 4"
              "|m_vv 72|m_rw 384|m_w 128|m_f 128|m_m 128|m_cc 136"),
        (I32, "pi 8|bi 8|bj 8"),
        (U16, "hl 2|lst0 8|lst1 8|lst2 8|lst3 8|bl0 2|bl1 4|bl2 4|bu 4|m_toff 4|m_fl 4")):
    for _n in _names.split("|"):
        SCRATCH[_n.split()[0]] = ("sbuf", [128, int(_n.split()[1])], _d)
for _n, _w in (("u", 128), ("e", 512), ("g", 256), ("w", 128), ("n", 128), ("x0", 144), ("x", 140), ("p", 128), ("h0", 256), ("h", 128)):
    SCRATCH["q" + _n] = ("sbuf", [128, _w], MX)
    SCRATCH["s" + _n] = ("sbuf", [128, _w], U8)
for _n, _w in [("z%d" % _b, 320) for _b in range(3)] + [("y3", 64)]:
    SCRATCH[_n] = ("sbuf", [128, _w], MX)
    SCRATCH["s" + _n] = ("sbuf", [128, _w], U8)
SCRATCH["hc"] = ("sbuf", [128, 64], MX)
SCRATCH["hs"] = ("sbuf", [128, 64], U8)
SCRATCH["PE"] = ("psum", [128, 2048], F32)
for _n in ("PR", "PC", "PL", "PS"):
    SCRATCH[_n] = ("psum", [128, 512], F32)

SEMAPHORES = (["kv", "ka", "kt", "kg", "sent", "hc", "hs", "hl", "st"] + ["al%d" % b for b in range(3)] + ["ac%d" % b for b in range(3)]
              + ["ld%d" % i for i in range(4)])

ORDER = {
    "v": "floor m4 pat0 ldz pat2 pf onesa pat3 pat1 phi ph128 ur0 ur1 ur2 ur3 plo qu qg0 onesb qg1 qx0 d0 wi0 d1 ac0 ac1 wi1 twi1 ht0 ht1 qh0 qh1 "
         "qe0 qe1 lst0 z0o qe2 qe3 pi15 off pm vvc jc mtz n4 huge xxz t1.0 rst mask zer xxl "
         "bi bj0 bj1 bu vv.0 pa0.0 g4.0 mt1.0 v.0 dxb.0 g5.0 mt2.0 mt0.0 mt3.0 mc.0 hc.0 fa.0 qm.0 cc.0 strike.0 fb.0 ga.0 f.0 fl.0 wa.0 "
         "m1.0 cca.0 ccb.0 xxn.0 rka.0 rkb.0 xxh.0 xxm.0 ht.0 qx.0 qh.0 zz1 daz cut lst1 z1o t1.1 da2.1 da3.1 "
         "g4.1 dxb.1 g5.1 vv.1 toff.1 fa.1 v.1 pa0.1 pa1.1 mt0.1 hc.1 mt2.1 mt1.1 mt3.1 mc.1 fb.1 qm.1 cc.1 strike.1 ga.1 xxn.1 f.1 fl.1 wa.1 "
         "m1.1 xxm.1 cca.1 ccb.1 rka.1 rkb.1 xxh.1 ht.1 qx.1 qh.1 zz2 qn lst2 z2o t1.2 da2.2 da3.2 qw "
         "g4.2 dxb.2 g5.2 vv.2 toff.2 fa.2 v.2 pa0.2 pa1.2 mt0.2 hc.2 mt2.2 mt1.2 mt3.2 mc.2 fb.2 qm.2 cc.2 strike.2 ga.2 f.2 fl.2 wa.2 "
         "m1.2 cca.2 ccb.2 rka.2 gt rkb.2 pt xxh.2 sel qp qx.2 ht.2 qh.2 lst3 y3o ys nbs",
    "a": "gr1 xa64 xa0 xa32 sc0 sr0 sc1 sr1 twi0 tac0 tac1 z0s "
         "nra.0 da0.0 da1.0 da2.0 da3.0 nca.0 pa1.0 pa2.0 pa3.0 nrb.0 eq.0 nc.0 wp.0 eq2.0 sc.0 wm.0 z1s "
         "nra.1 da0.1 da1.1 rw.1 nrb.1 nca.1 pa2.1 pa3.1 nc.1 eq.1 wp.1 eq2.1 sc.1 wm.1 z2s "
         "nra.2 da0.2 da1.2 rw.2 nrb.2 nca.2 pa2.2 pa3.2 nc.2 eq.2 wp.2 eq2.2 sc.2 wm.2 nrc yt y3s osc0 osc1 osc2 osc3",
    "t": "col0 row0 col1 row1 ls0_0 ls0_16 ls1_8 ls1_16 "
         "uo0.0 uo1.0 uo2.0 uo3.0 up0.0 up1.0 up2.0 up3.0 cp.0 rp.0 cm.0 rm.0 ls0.0 ls12.0 "
         "uo2.1 uo0.1 uo1.1 uo3.1 ro.1 up0.1 up1.1 up2.1 up3.1 cp.1 rp.1 cm.1 rm.1 ls0.1 ls12.1 "
         "uo2.2 uo0.2 uo1.2 uo3.2 ro.2 up0.2 up1.2 up2.2 up3.2 cp.2 rp.2 cm.2 rm.2 ymm pos ls0.2 ls12.2",
    "g": "pi ld0 hp zd iot sl0 sc_0 ss0 tz0 kr dxa.0 dgb rwz tz1 tz2 sl1 sc_1 ss1 dxa.1 ptz sl2 sc_2 ss2 dxa.2",
    "s": "ut gr0 wt oc y nb",
}


def make_flow(g, T):
    eng = {"v": g.vector, "a": g.scalar, "t": g.tensor, "g": g, "s": g.sync}
    own = {"v": "kv", "a": "ka", "t": "kt", "g": "kg"}
    calls, wr, rd = {}, {}, {}

    def note(name, q, kind, reads, writes, fn, args, kw):
        if name in calls:
            raise ValueError("twice " + name)
        raw, other = set(), set()
        for t in reads:
            raw.add(wr[t])
        for t in writes:
            if t in wr:
                other.add(wr[t])
            other.update(rd.get(t, ()))
        for t in reads:
            rd.setdefault(t, []).append(name)
        for t in writes:
            wr[t] = name
            rd[t] = []
        other.discard(name)
        calls[name] = (q, kind, raw, other, fn, args, kw)

    def op(name, q, reads, writes, fn, *args, **kw):
        note(name, q, "op", reads, writes, fn, args, kw)

    def dma(name, q, reads, writes, sem, out, in_):
        note(name, q, "dma", reads, writes, sem, (out, in_), {})

    def remote(name, reads, fn, *args):
        note(name, "g", "remote", reads, [], fn, args, {})

    def arrives(name, sem, val):
        note(name, None, "arrives", [], [name], sem, val, {})

    def issue():
        queue = {q: ORDER[q].split() for q in eng}
        for q in eng:
            if sorted(queue[q]) != sorted(n for n in calls if calls[n][0] == q):
                raise ValueError("the order of queue " + q)
        total, clock, event, known, age = {}, {k: {} for k in eng}, {}, {}, {}
        for n, c in calls.items():
            if c[1] == "arrives":
                event[n] = (c[4], c[5])
                known[n] = {c[4]: c[5]}
                age[n] = 0
                total[c[4]] = c[5]

        def need(q, names):
            for n in sorted(names, key=lambda n: (-age[n], n)):
                sem, val = event[n]
                if clock[q].get(sem, 0) >= val:
                    continue
                eng[q].wait_ge(T.sem[sem], val)
                for s, v in known[n].items():
                    clock[q][s] = max(clock[q].get(s, 0), v)

        while any(queue.values()):
            moved = False
            for q in eng:
                while queue[q] and all(d in age for d in calls[queue[q][0]][2] | calls[queue[q][0]][3]):
                    n = queue[q].pop(0)
                    kind, raw, other, fn, args, kw = calls[n][1:]
                    moved = True
                    age[n] = len(age) + 1
                    need(q, raw | {d for d in other if kind != "op" or calls[d][0] != q or calls[d][1] != "op"})
                    if kind == "remote":
                        fn(*args)
                        continue
                    sem, step = (own[q], 1) if kind == "op" else (fn, 16)
                    (fn(*args, **kw) if kind == "op" else eng[q].dma_start(*args)).then_inc(T.sem[sem], step)
                    total[sem] = total.get(sem, 0) + step
                    event[n] = (sem, total[sem])
                    known[n] = dict(clock[q])
                    known[n][sem] = total[sem]
            if not moved:
                raise ValueError("the queues wait for one another")
        return [(sem, val) for sem, val in total.items() if clock["g"].get(sem, 0) < val]

    return op, dma, remote, arrives, issue


def rank_program(g, core, T, topo):
    rank = T.rank_of(core)
    sent = [0]
    OWN, PARTNER = slice(64, 128), slice(128, 192)

    def engines(src, dst, away=None):
        return [x for x in topo.engines(src, dst) if away is None or x in topo.engines(src, away)]

    def send(out, in_, dst, sem, away=None):
        e = engines(core, dst, away)
        rid, pid = topo.addr(dst, core)
        g.remote_dma(out, in_, T.sem[sem], T.sem.sent, pid, rid, sum(1 << x for x in e))
        sent[0] += len(e)

    def helpers(r):
        c0, far = T.cores[r], T.cores[r ^ 1]
        hs = [c for c in topo.cores_of(c0) if c != c0 and topo.die(c) == topo.die(c0) and topo.may_write(c, far)]
        return hs[0], hs[-1]

    def bits(v):
        return v.bitcast(dt.uint8)

    if rank is None:
        for r in range(len(T.cores)):
            a, b = helpers(r)
            if core not in (a, b):
                continue
            far = T.cores[r ^ 1]
            n = len(engines(T.cores[r], core, T.cores[r ^ 2]))
            if core == b:
                g.wait_ge(T.sem.hl, n)
                send(T.bl0[:], T.hl[:], far, "al0")
            if core == a:
                g.wait_ge(T.sem.hc, n)
                send(bits(T.z0[:, PARTNER]), bits(T.hc[:]), far, "ac0")
            if core == b:
                g.wait_ge(T.sem.hs, n)
                send(T.sz0[:, PARTNER], T.hs[:], far, "ac0")
            g.wait_ge(T.sem.sent, sent[0])
        return

    op, dma, remote, arrives, issue = make_flow(g, T)
    V, A, PE = g.vector, g.scalar, g.tensor
    X = AxisListType.X
    loose = {"allow_small_or_imprecise_dtypes": True}
    pf, pm, off, huge, floor = [T.cst[:, i:i + 1] for i in range(5)]
    nc, nca, hit = [T.m_c[:, i:i + 1] for i in range(3)]
    hc, mc, cc, v = [T.m_v[:, i:i + 1] for i in range(4)]
    rk, rkb, sel = [T.m_r[:, i:i + 1] for i in range(3)]
    sc = T.m_sc[:, 0:1]

    def mm(name, reads, bank, out, left, a, right, b, n=128, start=True, stop=True):
        sl, sr = ["s" + (x[1:] if x[0] == "q" else x) for x in (left, right)]
        op(name, "t", reads, [bank], PE.matmul_mx, out, T[left][:, a:a + 128], T[sl][:, a:a + 128], T[right][:, b:b + n], T[sr][:, b:b + n], start, stop)

    op("floor", "v", [], ["floor"], V.memset, floor, FLOOR)
    dma("ut", "s", [], ["ut"], "ld0", T.ut[:, 0:4], T.u[:, 0:4])
    dma("gr0", "s", [], ["gr0"], "ld1", T.grt[:, 0:512], T.gr[:, 0:512])
    dma("gr1", "a", ["floor"], ["gr1"], "ld2", T.grt[:, 512:1024], T.gr[:, 512:1024])
    dma("wt", "s", ["gr1"], ["wt"], "ld3", T.wt[:], T.w[:])

    op("pi", "g", [], ["pi"], g.iota, T.pi[:, 0:1], [[0, 1]], 0, 1)
    op("ldz", "v", [], ["ldz"], V.memset, T.ldz[:], BELOW)
    op("m4", "v", [], ["m4"], V.memset, T.m4[:], MAGIC)
    op("onesa", "v", [], ["onesa"], V.memset, T.ones[:, 96:224], 1.0)
    op("onesb", "v", [], ["onesb"], V.memset, T.ones[:, 224:616], 1.0)
    op("pf", "v", ["pi"], ["pf"], V.tensor_copy, pf, T.pi[:, 0:1])
    op("phi", "v", ["m4", "pf"], ["phi"], V.tensor_scalar, T.phi[:], T.m4[:], pf, MAGIC, OP.add, OP.subtract)
    op("ph128", "v", ["m4", "pf"], ["ph128"], V.tensor_scalar, T.ph128[:], T.m4[:], pf, MAGIC - 128.0, OP.add, OP.subtract)
    op("plo", "v", ["phi", "pf"], ["plo"], V.tensor_scalar, T.plo[:], T.phi[:], pf, -1.0, OP.subtract, OP.mult)
    op("ld0", "g", ["ldz"], ["ld0"], g.affine_select, T.ld0[:], T.ldz[:], [[-1, 128]], OP.is_gt, 1.0, 0, 1)
    op("hp", "g", [], ["hp"], g.iota, T.hp[:], [[0, 8], [1, 16], [16, 4]], 0, 0, **loose)
    op("pat0", "v", [], ["pat0"], V.memset, T.pat[:], 0.0)
    for k, at, val in ((1, slice(0, 16, 5), 1.0), (2, slice(16, 22, 5), 1.0), (3, slice(18, 24, 5), 256.0)):
        op("pat%d" % k, "v", ["pat0"], ["pat%d" % k], V.memset, T.pat[:, at], val)
    for i, src in ((0, "phi"), (32, "ph128"), (64, "plo")):
        op("xa%d" % i, "a", [src, "pat1", "pat2", "pat3"], ["xa%d" % i], A.activation, T.ones[:, i:i + 32], T.pat[:], AF.Copy, scale=T[src][:, 0:1])
    op("qx0", "v", ["xa0", "xa32", "xa64", "onesa", "onesb"], ["qx0"], V.quantize_mx, T.qx0[:], T.sx0[:], T.ones[:, 0:576])
    for t in range(4):
        op("ur%d" % t, "v", ["onesa", "ut"], ["ur%d" % t], V.tensor_scalar, T.ur[:, t:512:4], T.ones[:, 96:224], T.ut[:, t:t + 1], None, OP.mult)
    H = [slice(0, 128), slice(128, 256)]
    op("qu", "v", ["ur0", "ur1", "ur2", "ur3"], ["qu"], V.quantize_mx, T.qu[:], T.su[:], T.ur[:])
    op("qg0", "v", ["gr0"], ["qg0"], V.quantize_mx, T.qg[:, H[0]], T.sg[:, H[0]], T.grt[:, 0:512])
    op("qg1", "v", ["gr1"], ["qg1"], V.quantize_mx, T.qg[:, H[1]], T.sg[:, H[1]], T.grt[:, 512:1024])
    for h, P in ((0, "PC"), (1, "PS")):
        mm("col%d" % h, ["qu", "qg%d" % h], P, T[P][:, 0:128], "qg", 128 * h, "qu", 0)
        mm("row%d" % h, ["qu", "qg%d" % h], "PE%d" % h, T.PE[:, 512 * h:512 * h + 128], "qu", 0, "qg", 128 * h)
        op("sc%d" % h, "a", [P, "floor"], ["sc%d" % h], A.activation, T.sc0[:, h:h + 1], T[P][:, 0:1], AF.Abs, bias=floor)
        op("sr%d" % h, "a", ["PE%d" % h, "floor"], ["sr%d" % h], A.activation, T.sr0[:, H[h]], T.PE[:, 512 * h:512 * h + 128], AF.Abs, bias=floor)
        op("d%d" % h, "v", ["ld0", "sc%d" % h], ["d%d" % h], V.tensor_scalar, T["d%d" % h][:], T.ld0[:], T.sc0[:, h:h + 1], None, OP.mult)
    for h in range(2):
        op("wi%d" % h, "v", ["sr%d" % h, "d%d" % h], ["wi%d" % h], V.tensor_tensor, T["c%d" % h][:, H[h]], T.sr0[:, H[h]], T["d%d" % h][:], OP.is_gt)
        op("ac%d" % h, "v", ["sr%d" % (1 - h), "sc%d" % h], ["ac%d" % h], V.tensor_scalar,
           T["c%d" % h][:, H[1 - h]], T.sr0[:, H[1 - h]], T.sc0[:, h:h + 1], None, OP.is_ge if h else OP.is_gt)
        for k, part, i in (("ac", H[1 - h], 2 * h), ("wi", H[h], 2 * h + 1)):
            name = "t%s%d" % (k, h)
            if name == "twi1":
                op(name, "v", [k + str(h)], [name], V.tensor_reduce, T.rk0[:, i:i + 1], T["c%d" % h][:, part], X, OP.add)
            else:
                op(name, "a", [k + str(h)], [name], A.activation, T["c%d" % (h + 2)][:, part], T["c%d" % h][:, part], AF.Copy, accum_out=T.rk0[:, i:i + 1])
        op("ht%d" % h, "v", ["hp", "tac%d" % h, "twi%d" % h], ["ht%d" % h], V.tensor_scalar,
           T.ht0[:, 512 * h:512 * h + 512], T.hp[:], T.rk0[:, 2 * h:2 * h + 1], T.rk0[:, 2 * h + 1:2 * h + 2], OP.subtract, OP.is_equal)
        op("qh%d" % h, "v", ["ht%d" % h], ["qh%d" % h], V.quantize_mx, T.qh0[:, H[h]], T.sh0[:, H[h]], T.ht0[:, 512 * h:512 * h + 512])
        for c in (8 * h, 16):
            mm("ls%d_%d" % (h, c), ["qh%d" % h, "qx0"], "PL", T.PL[:, 0:128], "qh0", 128 * h, "qx0", c, 128, h == 0 and c == 0, h == 1 and c == 16)
    op("lst0", "v", ["PL"], ["lst0"], V.tensor_copy, T.lst0[:, 0:6], T.PL[:, 0:6])
    op("zer", "v", [], ["zer"], V.memset, T.zer[:], 0.0)
    for b in (1, 2):
        op("zz%d" % b, "v", ["zer"], ["z%dz" % b], V.quantize_mx, T["z%d" % b][:, 0:128], T["sz%d" % b][:, 0:128], T.zer[:])

    def pick(b, into, at):
        src, ssrc, w, frm = (("qg", "sg", slice(0, 256), ["qg0", "qg1"]) if b == 0 else
                             ("z%d" % (b - 1), "sz%d" % (b - 1), slice(64, 256), ["z%d%s" % (b - 1, k) for k in "psom"]))
        lst = "lst%d" % b
        frm = frm + [lst] + ([into + "z"] if b in (1, 2) else [])
        op(into + "o", "v", frm, [into + "o"], V.tensor_copy,
           T[into][:, at].bitcast(dt.uint32), T[src][:, w].bitcast(dt.uint32).indirect(T[lst][:, 0:4]))
        op(into + "s", "a", frm, [into + "s"], A.activation, T["s" + into][:, at], T[ssrc][:, w].indirect(T[lst][:, 0:4]), AF.Copy)

    ha, hb = helpers(rank)
    away = T.cores[rank ^ 2]
    remote("sl0", ["lst0"], send, T.hl[:], T.lst0[:, 4:6], hb, "hl", away)
    pick(0, "z0", OWN)
    remote("sc_0", ["z0o"], send, bits(T.hc[:]), bits(T.z0[:, OWN]), ha, "hc", away)
    remote("ss0", ["z0s"], send, T.hs[:], T.sz0[:, OWN], hb, "hs", away)

    op("zd", "g", ["onesa", "onesb"], ["zd"], g.affine_select, T.zd[:, 0:516], T.ones[:, 96:612], [[-1, 516]], OP.is_equal, 0.0, 3, 4)
    op("iot", "g", [], ["iot"], g.iota, T.iot[:], [[1, 256]], 0, 0, **loose)
    op("kr", "g", [], ["kr"], g.iota, T.kr[:], [[0, 4], [1, 16]], 0, 0, **loose)
    op("dgb", "g", ["onesa"], ["dgb"], g.affine_select, T.dgb[:], T.ones[:, 96:160], [[-1, 64]], OP.is_equal, 0.0, -64, 1)
    for b in range(3):
        op("tz%d" % b, "g", [], ["t1%d" % b], g.iota, T["t1%d" % b][:], [[1, 256]], 128, 0, **loose)
    op("ptz", "g", [], ["ptz"], g.iota, T.pt[:], [[0, 512]], 0, 0, **loose)
    op("rwz", "g", [], ["rwz"], g.iota, T.m_rw[:, 64:384], [[0, 320]], 0, 0, **loose)
    for t in range(4):
        op("qe%d" % t, "v", ["zd"], ["qe%d" % t], V.quantize_mx, T.qe[:, 128 * t:128 * t + 128], T.se[:, 128 * t:128 * t + 128], T.zd[:, 3 - t:515 - t])
    op("daz", "v", [], ["daz"], V.memset, T.m_da[:, 256:576], 0.0)
    op("pi15", "v", ["pi"], ["pi15"], V.tensor_scalar, T.pi[:, 1:2], T.pi[:, 0:1], 15, None, OP.bitwise_and)
    op("pm", "v", ["pi15"], ["pm"], V.tensor_copy, pm, T.pi[:, 1:2])
    op("rst", "v", ["kr"], ["rst"], V.tensor_scalar, T.rst[:], T.kr[:], 0.5, None, OP.is_gt)
    op("mask", "v", ["kr", "pm"], ["mask"], V.tensor_scalar, T.mask[:], T.kr[:], pm, None, OP.is_equal)
    op("jc", "v", ["hp", "pm"], ["jc"], V.tensor_scalar, T.jc[:], T.hp[:, 0:4], pm, None, OP.add)
    op("vvc", "v", ["pf"], ["vvc"], V.tensor_scalar, T.m_vv[:, 64:65], pf, 63.5, BIG, OP.is_lt, OP.mult)
    op("n4", "v", [], ["n4"], V.memset, T.n4[:], 64.0)
    op("cut", "v", [], ["cut"], V.memset, T.m_cc[:, 64:65], -63.5)
    op("off", "v", ["pf"], ["off"], V.tensor_scalar, off, pf, 63.5, -16.0, OP.is_gt, OP.mult)
    op("huge", "v", [], ["huge"], V.memset, huge, HUGE)
    op("mtz", "v", [], ["mtz"], V.memset, T.m_mt[:, 256:512], 0.0)
    op("xxz", "v", [], ["xxz"], V.memset, T.xx[:], 0.0)
    op("xxl", "v", ["plo", "xxz"], ["xxl"], V.tensor_copy, T.xx[:, 48:64:5], T.plo[:])
    op("qn", "v", ["onesa", "onesb"], ["qn"], V.quantize_mx, T.qn[:], T.sn[:], T.ones[:, 96:608])
    op("qw", "v", ["wt"], ["qw"], V.quantize_mx, T.qw[:], T.sw[:], T.wt[:])

    for b in range(3):
        nx, B = b + 1, ".%d" % b
        zn = "z%d" % b
        z, sz = T[zn], T["s" + zn]
        own, mrg, prt = [zn + "o", zn + "s"], zn + "m", zn + "p"
        t1 = "t1%d" % b
        aw, awt = (T.lst0[:, 0:4], "lst0") if b == 0 else (T["lst%d" % b][:, 4:8], "lst%d" % b)

        op("t1" + B, "v", ["iot", awt, t1], [t1], V.tensor_copy, T[t1][:].indirect(aw), T.iot[:, 0:64])
        op("nra" + B, "a", ["iot", awt], ["nra"], A.activation, T.m_nr[:, 0:64], T.iot[:].indirect(aw), AF.Copy)
        op("dxa" + B, "g", ["nra"], ["dxa"], g.affine_select, T.m_dx[:, 0:64], T.m_nr[:, 0:64], [[-1, 64]], OP.is_equal, 0.0, 0, 1)
        op("nca" + B, "a", ["dxa", "off"], ["nca", "dya"], A.activation, T.m_dy[:, 128:192], T.m_dx[:, 0:64], AF.Identity, bias=off, accum_out=nca)
        for t in range(4):
            if b == 0:
                mm("uo%d" % t + B, ["qe%d" % t, "qg0", "qg1"], "PE%d" % t, T.PE[:, 512 * t:512 * t + 256], "qe", 128 * t, "qg", 0, 256)
                op("da%d" % t + B, "a", ["PE%d" % t], ["dn%d" % t], A.activation, T.m_dn[:, 256 * t:256 * t + 256], T.PE[:, 512 * t:512 * t + 256], AF.Copy)
                continue
            mm("uo%d" % t + B, ["qe%d" % t, zn + "z"] + own, "PE%d" % t, T.PE[:, 512 * t:512 * t + 128], "qe", 128 * t, zn, 0)
            plane, bank = T.m_da[:, 64 * t:64 * t + 64], T.PE[:, 512 * t + 64:512 * t + 128]
            if t < 2:
                op("da%d" % t + B, "a", ["PE%d" % t], ["da%d" % t], A.activation, plane, bank, AF.Copy)
            else:
                op("da%d" % t + B, "v", ["PE%d" % t], ["da%d" % t], V.tensor_copy, plane, bank)
        if b:
            mm("ro" + B, ["qu", zn + "z"] + own, "PR", T.PR[:, 0:128], "qu", 0, zn, 0)
            op("rw" + B, "a", ["PR", "floor"], ["rw"], A.activation, T.m_rw[:, 0:64], T.PR[:, 64:128], AF.Abs, bias=floor)

        src = helpers(rank ^ 1)[0] if b == 0 else T.cores[rank ^ (1 << b)]
        n = len(topo.engines(src, core))
        arrives("bl%d" % b, "al%d" % b, n)
        arrives(prt, "ac%d" % b, 2 * n)

        if b == 0:
            op("bi", "v", ["bl0"], ["bi"], V.tensor_copy, T.bi[:, 0:2], T.bl0[:])
            op("bj0", "v", ["bi"], ["bj0"], V.tensor_scalar, T.bj[:, 0:2], T.bi[:, 0:2], 255, None, OP.bitwise_and)
            op("bj1", "v", ["bi"], ["bj1"], V.tensor_scalar, T.bj[:, 2:4], T.bi[:, 0:2], 8, None, OP.logical_shift_right)
            op("bu", "v", ["bj0", "bj1"], ["bu"], V.tensor_copy, T.bu[:], T.bj[:, 0:4])
        bwt = "bl%d" % b if b else "bu"
        bw = T[bwt][:]
        op("g4" + B, "v", [t1, bwt, "mask"], ["g4"], V.tensor_tensor, T.m_g4[:], T[t1][:].indirect(bw), T.mask[:], OP.mult)
        op("g5" + B, "v", ["g4", "rst"], ["g5"], V.tensor_tensor_scan, T.m_g5[:], T.rst[:], T.m_g4[:], 0.0, OP.mult, OP.add)
        if b:
            op("toff" + B, "v", ["g5"], ["toff"], V.tensor_copy, T.m_toff[:], T.m_g5[:, 15:64:16])
        op("fa" + B, "v", ["g5"], ["fa"], V.tensor_scalar, T.m_fa[:], T.m_g5[:, 15:64:16], 63.5, 64.0, OP.is_lt, OP.mult)
        op("vv" + B, "v", [t1, bwt, "dgb"], ["vv"], V.tensor_tensor, T.m_vv[:, 0:64], T[t1][:].indirect(bw), T.dgb[:], OP.mult)
        op("v" + B, "v", ["vv", "vvc"], ["v"], V.tensor_reduce, v, T.m_vv[:, 0:65], X, OP.add)
        op("nrb" + B, "a", ["iot", bwt], ["nrb"], A.activation, T.m_nr[:, 64:128], T.iot[:].indirect(bw), AF.Copy)
        op("dxb" + B, "v", ["iot", bwt, "dgb"], ["dxb"], V.tensor_tensor, T.m_dx[:, 64:128], T.iot[:].indirect(bw), T.dgb[:], OP.mult)
        op("nc" + B, "a", ["dxa", "dxb"], ["nc", "dy"], A.activation, T.m_dy[:, 0:128], T.m_dx[:], AF.Copy, accum_out=nc)
        for t in range(4):
            pa = T.m_pa[:, 64 * t:64 * t + 64]
            if b == 0:
                da, frm = T.m_dn[:, 256 * t:256 * t + 256].indirect(bw), ["dn%d" % t, bwt]
            else:
                da, frm = T.m_da[:, 64 * t:64 * t + 384].indirect(T.m_toff[:]), ["da%d" % k for k in range(t, 4)] + ["daz", "toff"]
            if t < (2 if b else 1):
                op("pa%d" % t + B, "v", frm, ["pa%d" % t], V.tensor_copy, pa, da)
            else:
                op("pa%d" % t + B, "a", frm, ["pa%d" % t], A.activation, pa, da, AF.Copy)
        op("fb" + B, "v", ["fa", "jc"], ["fb"], V.tensor_tensor, T.m_fb[:], T.m_fa[:], T.jc[:], OP.add)
        op("fl" + B, "v", ["fb"], ["fl"], V.tensor_copy, T.m_fl[:], T.m_fb[:])
        op("mc" + B, "v", ["v"], ["mc"], V.tensor_scalar, mc, v, 63.5, None, OP.is_lt)
        op("hc" + B, "v", ["v"], ["hc"], V.tensor_scalar, hc, v, 63.5, None, OP.is_gt)
        op("xxh" + B, "v", ["phi", "n4", "mc", "xxz"], ["xxh"], V.tensor_scalar, T.xx[:, 0:16:5], T.n4[:], mc, T.phi[:, 0:1], OP.mult, OP.add)
        if b < 2:
            op("xxn" + B, "v", ["m4", "nc", "xxz"], ["xxn"], V.tensor_scalar, T.xx[:, 16:32:5], T.m4[:], nc, MAGIC, OP.add, OP.subtract)
            op("xxm" + B, "v", ["xxn", "nc"], ["xxm"], V.tensor_scalar, T.xx[:, 64:80:5], T.xx[:, 16:32:5], nc, -1.0, OP.subtract, OP.mult)
        op("qx" + B, "v", ["xxl", "xxh"] + (["xxn", "xxm"] if b < 2 else []), ["qx"], V.quantize_mx, T.qx[:], T.sx[:], T.xx[:])
        op("eq" + B, "a", ["iot", bwt, "nca"], ["eq"], A.activation, T.m_eq[:], T.iot[:].indirect(bw), AF.Abs, bias=nca, scale=-1.0)
        op("eq2" + B, "a", ["eq", "huge"], ["hit", "eq2"], A.activation, T.m_eq2[:], T.m_eq[:], AF.Relu, bias=huge, scale=-HUGE, accum_out=hit)
        if b == 0:
            op("strike" + B, "v", ["sr0", "sr1", "zer", bwt], ["sr0", "sr1", "rw"], V.tensor_copy, T.sr0[:].indirect(bw), T.zer[:, 0:64])
        else:
            op("strike" + B, "v", ["rw", "rwz", "zer", "toff"], ["rw"], V.tensor_copy, T.m_rw[:].indirect(T.m_toff[:]), T.zer[:, 0:64])
        op("ga" + B, "v", ["nra", "nc"], ["ga"], V.tensor_scalar, T.m_f[:, 0:64], T.m_nr[:, 0:64], nc, BELOW, OP.is_lt, OP.max)
        op("wa" + B, "v", ["rw", "ga", awt], ["wa"], V.tensor_tensor, T.m_m[:, 0:64], T.m_rw[:, 0:64] if b else T.sr0[:].indirect(aw),
           T.m_f[:, 0:64], OP.mult)
        op("f" + B, "v", ["nrb", "nc"], ["f"], V.tensor_scalar, T.m_f[:, 64:128], T.m_nr[:, 64:128], nc, BELOW, OP.is_ge, OP.max)

        for t in range(4):
            mm("up%d" % t + B, ["qe%d" % t, prt] + own, "PE%d" % t, T.PE[:, 512 * t:512 * t + 128], "qe", 128 * t, zn, 64)
            op("mt%d" % t + B, "v", ["PE%d" % t, "pa%d" % t], ["mt%d" % t], V.tensor_tensor,
               T.m_mt[:, t:256:4], T.PE[:, 512 * t + 64:512 * t + 128], T.m_pa[:, 64 * t:64 * t + 64], OP.add)
        mm("cp" + B, ["qu", prt] + own, "PL", T.PL[:, 0:128], zn, 64, "qu", 0)
        mm("rp" + B, ["qu", prt] + own, "PR", T.PR[:, 0:128], "qu", 0, zn, 64)
        op("wp" + B, "a", ["PR", "floor"], ["wp"], A.activation, T.m_w[:, 0:64], T.PR[:, 64:128], AF.Abs, bias=floor)
        op("cc" + B, "v", ["PL", "hc"], ["cc"], V.tensor_scalar, cc, T.PL[:, 0:1], hc, FLOOR, OP.mult, OP.add)
        op("qm" + B, "v", ["mt0", "mt1", "mt2", "mt3", "mtz"], [mrg], V.quantize_mx, z[:, 192:320], sz[:, 192:320], T.m_mt[:])

        mm("cm" + B, ["qu", mrg, prt], "PC", T.PC[:, 0:128], zn, 128, "qu", 0)
        mm("rm" + B, ["qu", mrg, prt], "PS", T.PS[:, 0:128], "qu", 0, zn, 128)
        op("sc" + B, "a", ["PC", "mc", "cc"], ["sc"], A.activation, sc, T.PC[:, 0:1], AF.Abs, bias=cc, scale=mc)
        op("wm" + B, "a", ["PS", "floor"], ["wm"], A.activation, T.m_w[:, 64:128], T.PS[:, 64:128], AF.Abs, bias=floor)
        op("m1" + B, "v", ["f", "sc", "hit"], ["m1"], V.tensor_scalar, T.m_m[:, 64:128], T.m_f[:, 64:128], sc, hit, OP.mult, OP.subtract)
        op("cca" + B, "v", ["wa", "sc"], ["cca"], V.tensor_scalar, T.m_cc[:, 0:64], T.m_m[:, 0:64], sc, None, OP.is_ge)
        op("ccb" + B, "v", ["wp", "wm", "fl", "m1"], ["ccb"], V.tensor_tensor, T.m_cc[:, 72:136], T.m_w[:].indirect(T.m_fl[:]), T.m_m[:, 64:128], OP.is_gt)
        if b < 2:
            op("rka" + B, "v", ["cca"], ["rka"], V.tensor_reduce, rk, T.m_cc[:, 0:64], X, OP.add)
            op("rkb" + B, "v", ["ccb"], ["rkb"], V.tensor_reduce, rkb, T.m_cc[:, 72:136], X, OP.add)
            op("ht" + B, "v", ["hp", "rka", "rkb"], ["ht"], V.tensor_scalar, T.m_ht[:], T.hp[:], rk, rkb, OP.subtract, OP.is_equal)
        else:
            op("gt", "v", ["nra", "nrb", "nc"], ["gt"], V.tensor_scalar, T.m_gt[:], T.m_nr[:, 0:128], nc, BIG, OP.is_le, OP.mult)
            op("rka" + B, "v", ["cca", "cut"], ["rka"], V.tensor_reduce, rk, T.m_cc[:, 0:65], X, OP.add)
            op("rkb" + B, "v", ["ccb"], ["rkb"], V.tensor_reduce, rkb, T.m_cc[:, 72:136], X, OP.add, negate=True)
            op("pt", "v", ["gt", "rka", "rkb", "ptz"], ["pt"], V.tensor_scalar, T.pt[:, 0:512:4], T.m_gt[:], rk, rkb, OP.add, OP.is_lt)
            op("sel", "v", ["rka", "rkb"], ["sel"], V.tensor_scalar, sel, rk, rkb, None, OP.is_lt)
            op("qp", "v", ["pt"], ["qp"], V.quantize_mx, T.qp[:], T.sp[:], T.pt[:])
            mm("pos", ["qp", "qn"], "PC", T.PC[:, 0:128], "qp", 0, "qn", 0)
            op("ht" + B, "v", ["hp", "PC", "sel"], ["ht"], V.tensor_scalar, T.m_ht[:], T.hp[:], T.PC[:, 0:1], sel, OP.is_equal, OP.mult)
            mm("ymm", ["qw", mrg, prt] + own, "PE0", T.PE[:, 0:192], "qw", 0, zn, 64, 192)
            op("yt", "a", ["PE0"], ["yt"], A.activation, T.ytab[:], T.PE[:, 0:192], AF.Copy)
            op("nrc", "a", ["nrb"], ["nrc"], A.activation, T.m_nr[:, 128:192], T.m_nr[:, 64:128], AF.Copy)
        op("qh" + B, "v", ["ht"], ["qh"], V.quantize_mx, T.qh[:], T.sh[:], T.m_ht[:])
        for c in (0, 12):
            mm("ls%d" % c + B, ["qh", "qx"], "PL", T.PL[:, 0:128], "qh", 0, "qx", c, 128, c == 0, c == 12)
        lst = "lst%d" % nx
        k = 8 if b < 2 else 4
        op(lst, "v", ["PL"], [lst], V.tensor_copy, T[lst][:, 0:k], T.PL[:, 0:k])
        if b < 2:
            to = T.cores[rank ^ (1 << nx)]
            o = "z%d" % nx
            remote("sl%d" % nx, [lst], send, T["bl%d" % nx][:], T[lst][:, 4:8], to, "al%d" % nx)
            pick(nx, o, OWN)
            remote("sc_%d" % nx, [o + "o"], send, bits(T[o][:, PARTNER]), bits(T[o][:, OWN]), to, "ac%d" % nx)
            remote("ss%d" % nx, [o + "s"], send, T["s" + o][:, PARTNER], T["s" + o][:, OWN], to, "ac%d" % nx)

    pick(3, "y3", slice(0, 64))
    dma("oc", "s", ["y3o"], [], "st", T.oc[:], bits(T.y3[:]))
    op("ys", "v", ["yt", "lst3"], ["ys"], V.tensor_copy, T.ys[:], T.ytab[:].indirect(T.lst3[:, 0:4]))
    op("nbs", "v", ["nra", "nrb", "nrc", "lst3"], ["nbs"], V.tensor_copy, T.nbs[:], T.m_nr[:].indirect(T.lst3[:, 0:4]))
    for k in range(4):
        dma("osc%d" % k, "a", ["y3s"], [], "st", T.osc[4 * k:4 * k + 4, :], T.sy3[32 * k:32 * k + 4, :])
    dma("y", "s", ["ys"], [], "st", T.y[:], T.ys[:])
    dma("nb", "s", ["nbs"], [], "st", T.nb[:], T.nbs[0:1, :])
    left = issue()
    g.wait_ge(T.sem.sent, sent[0])
    for sem, val in sorted(left, key=lambda x: x[0] == "st"):
        g.wait_ge(T.sem[sem], val)
